import numpy as np
import ml_dtypes


def mxq(x, axis, fmt="e4m3"):
    dtype, down = {"e4m3": (ml_dtypes.float8_e4m3fn, 7), "e5m2": (ml_dtypes.float8_e5m2, 14)}[fmt]
    v = np.moveaxis(np.asarray(x, np.float32).astype(ml_dtypes.bfloat16).astype(np.float64), axis, -1)
    blocks = v.reshape(v.shape[:-1] + (-1, 32))
    amax = np.abs(blocks).max(-1, keepdims=True)
    byte = np.maximum(np.where(amax > 0, np.frexp(amax)[1] - 1 + 127, 0) - down, 1)
    scale = np.exp2(byte - 127.0)
    codes = (blocks / scale).astype(np.float32).astype(dtype).astype(np.float64)
    return np.moveaxis((codes * scale).reshape(v.shape), -1, axis)


WIDE = False


def mx_kscale(k):
    if not WIDE:
        return np.ones(k)
    levels = np.array([10, -10, 5, -5, 0])
    if k % 512:
        return np.exp2(np.random.permutation(np.resize(levels, k // 32))).repeat(32)
    a = np.empty((k // 512, 16))
    for p in range(k // 512):
        a[p, :8] = np.random.permutation(np.resize(levels, 8))
        for g in range(8):
            far = levels[np.abs(levels - a[p, g]) >= 10]
            a[p, g + 8] = far[np.random.randint(len(far))]
    return np.exp2(a.ravel()).repeat(32)


def f64(x):
    return np.asarray(x).astype(np.float64)


def striped(idx):
    return np.tile(idx.reshape(-1, 16).T, (8, 1)).astype(np.uint16)


def unstriped(offs):
    return offs[:16].T.reshape(-1).astype(np.int64)


E2M1 = np.array([0.0, 0.5, 1.0, 1.5, 2.0, 3.0, 4.0, 6.0, -0.0, -0.5, -1.0, -1.5, -2.0, -3.0, -4.0, -6.0])


def pack_weight(w, fmt):
    k, n = w.shape
    w = f64(np.asarray(w, np.float32).astype(ml_dtypes.bfloat16)).reshape(k // 32, 32, n)
    amax = np.abs(w).max(1)
    if fmt == "e4m3":
        byte = np.frexp(amax)[1] - 1 + 127 - 7
    else:
        mant, ex = np.frexp(amax / 6.0)
        byte = np.where(mant > 0.5, ex, ex - 1) + 127
    byte = np.clip(np.where(amax > 0, byte, 1), 1, 254)
    scaled = (w * np.exp2(127.0 - byte)[:, None, :]).reshape(k, n).astype(np.float32)
    by_word = np.ascontiguousarray(scaled.reshape(k // 512, 128, 4, n).transpose(0, 1, 3, 2))
    if fmt == "e4m3":
        words = by_word.astype(ml_dtypes.float8_e4m3fn).view(np.uint8)
    else:
        c = by_word.astype(ml_dtypes.float4_e2m1fn).view(np.uint8) & 0xF
        words = (c[..., 0::2] | (c[..., 1::2] << 4)).reshape(k // 512, 128, 2 * n)
    return np.ascontiguousarray(words), np.ascontiguousarray(byte.astype(np.uint8).reshape(k // 512, 16, n))


def unpack_weight(words, scales, fmt):
    g, _, n = scales.shape
    words = np.ascontiguousarray(words).reshape(g, 128, n, -1)
    if fmt == "e4m3":
        vals = words.view(ml_dtypes.float8_e4m3fn).astype(np.float64)
    else:
        nib = np.empty((g, 128, n, 4), np.uint8)
        nib[..., 0::2] = words & 0xF
        nib[..., 1::2] = words >> 4
        vals = E2M1[nib]
    vals = vals * np.repeat(np.exp2(scales.astype(np.float64) - 127.0), 8, axis=1)[..., None]
    return vals.transpose(0, 1, 3, 2).reshape(g * 512, n)


K, M, T, S = 512, 256, 2048, 1024


def setup_inputs():
    n = np.random.standard_normal
    s = mx_kscale(K)[:, None]
    s2 = mx_kscale(512)[:, None]
    v = pack_weight(n((K, T)) * s, "e4m3")
    p_w4 = pack_weight(n((K, M)) / np.sqrt(K) / s, "e2m1")
    return {
        "tab_words": v[0],
        "tab_scales": v[1],
        "w4_words": p_w4[0],
        "w4_scales": p_w4[1],
        "c": (n((512, S)) * s2).astype(np.float32),
        "u": (n((512, M)) / np.sqrt(512) / s2).astype(np.float32),
        "ts": np.tile(np.exp(0.5 * n(T)), (128, 1)).astype(np.float32),
        "b": (0.3 * n(256)).astype(np.float32),
        "offs": striped(np.random.permutation(T)[:S]),
    }


def reference(tab_words, tab_scales, w4_words, w4_scales, c, u, ts, b, offs):
    tab_ = unpack_weight(tab_words, tab_scales, "e4m3")[:, unstriped(offs)]
    w4_ = unpack_weight(w4_words, w4_scales, "e2m1")
    c_ = mxq(f64(c), 0, "e4m3")
    u_ = mxq(f64(u), 0, "e4m3")
    y = w4_.T @ tab_ + u_.T @ c_
    y = y * f64(ts)[0][unstriped(offs)]
    return y + f64(b)[:, None]

@@ -1,0 +1,171 @@
+from contextlib import ExitStack
+
+import concourse.mybir as mybir
+
+K, M, T, S = 512, 256, 2048, 1024
+FLOPS = 2 * 2 * K * M * S
+
+F32 = mybir.dt.float32
+BF16 = mybir.dt.bfloat16
+I32 = mybir.dt.int32
+U32 = mybir.dt.uint32
+U16 = mybir.dt.uint16
+U8 = mybir.dt.uint8
+FP8X4 = mybir.dt.float8_e4m3fn_x4
+FP4X4 = mybir.dt.float4_e2m1fn_x4
+MULT = mybir.AluOpType.mult
+IDENT = mybir.ActivationFunctionType.Identity
+
+P = 128
+PACK = 4
+HALVES = M // P
+CHUNK = 256
+C_LOADS = (256, 256, 256, 256)
+GATHER = 512
+TS_ROW = T // P
+BANK = 512
+
+
+def load_scale_rows(queues, plane, rows):
+    for q in range(4):
+        queues[q % len(queues)].dma_start(out=plane[32 * q : 32 * q + 4, :].bitcast(I32), in_=rows[4 * q : 4 * q + 4, :].bitcast(I32))
+
+
+def interleave(nc, grouped, raw):
+    nc.scalar.copy(
+        out=grouped.rearrange("p (c i) t -> p c t i", i=4),
+        in_=raw.rearrange("p t (c i) -> p c t i", i=4),
+    )
+
+
+def tile_list_tabts_bias_kernel(tc, tab_words, tab_scales, w4_words, w4_scales, c, u, ts, b, offs, out):
+    nc = tc.nc
+    with ExitStack() as ctx:
+        keep = ctx.enter_context(tc.tile_pool(name="keep", bufs=1))
+        late = ctx.enter_context(tc.tile_pool(name="late", bufs=1))
+        psum = ctx.enter_context(tc.psum_pool(name="psum", bufs=1))
+
+        offsets = keep.tile([P, S // 16], U16, name="offsets")
+        nc.sync.dma_start(offsets[:], offs)
+
+        ts_rows = keep.tile([P, TS_ROW], F32, name="ts_rows")
+        nc.sync.dma_start(out=ts_rows[:], in_=ts[0].rearrange("(p i) -> p i", i=TS_ROW))
+
+        u_raw = keep.tile([P, PACK, M], F32, name="u_raw")
+        nc.sync.dma_start(out=u_raw[:], in_=u.rearrange("(p t) n -> p t n", t=PACK))
+
+        table_scales = keep.tile([P, T], U8, name="table_scales", align_bytes=64)
+        nc.gpsimd.memset(table_scales[:].bitcast(I32), 0)
+        load_scale_rows((nc.sync, nc.scalar), table_scales, tab_scales[0])
+
+        zeros = late.tile([P, P], F32, name="zeros", offset=4 * T - 256)
+        nc.gpsimd.memset(zeros[:], 0.0)
+        ident = keep.tile([P, P], F32, name="ident")
+        nc.gpsimd.affine_select(
+            out=ident[:], in_=zeros[:], pattern=[[-1, P]], compare_op=mybir.AluOpType.not_equal,
+            fill=1.0, base=0, channel_multiplier=1,
+        )
+
+        table_words = late.tile([P, T], I32, name="table_words", align_bytes=64, offset=0)
+        nc.sync.dma_start(out=table_words[:], in_=tab_words[0].rearrange("p t i -> p (t i)").bitcast(I32))
+
+        raw = late.tile([P, PACK * S + HALVES], F32, name="raw", offset=4 * T)
+        bias = raw[:, PACK * S : PACK * S + HALVES]
+        w4 = keep.tile([P, 3 * M], U8, name="w4", align_bytes=64)
+        w4_codes = w4[:, 0 : 2 * M]
+        w4_plane = w4[:, 2 * M : 3 * M]
+
+        c_rows = c.rearrange("(p t) j -> p t j", t=PACK)
+        c_raw = []
+        start = 0
+        for n, width in enumerate(C_LOADS):
+            if n == len(C_LOADS) - 1:
+                nc.gpsimd.memset(w4[:].bitcast(I32), 0)
+                nc.sync.dma_start(out=w4_codes.bitcast(I32), in_=w4_words[0].bitcast(I32))
+                load_scale_rows((nc.sync,), w4_plane, w4_scales[0])
+            part = raw[:, PACK * start : PACK * (start + width)].rearrange("p (t j) -> p t j", t=PACK)
+            nc.sync.dma_start(out=part, in_=c_rows[:, :, start : start + width])
+            for j0 in range(0, width, CHUNK):
+                c_raw.append(part[:, :, j0 : j0 + CHUNK])
+            start = start + width
+        with nc.allow_non_contiguous_dma(reason="one bias value for each partition"):
+            nc.sync.dma_start(out=bias, in_=b.rearrange("(h p) -> p h", p=P))
+
+        ts_all = keep.tile([P, T], F32, name="ts_all")
+        ts_groups = ts_all[:].rearrange("m (p g i) -> m g p i", g=4, i=4)
+        for g in range(4):
+            spread = psum.tile([P, 4, P], F32, name=f"spread{g}")
+            for i in range(4):
+                col = 4 * g + i
+                nc.tensor.transpose(spread[:, i, :], ts_rows[:, col : col + 1].to_broadcast([P, P]), ident[:])
+            nc.scalar.copy(out=ts_groups[:, g], in_=spread[:].rearrange("m i p -> m p i"))
+
+        picked_scales = []
+        picked_words = []
+        picked_ts = []
+        for n in range(S // GATHER):
+            lst = offsets[:, n * GATHER // 16 : (n + 1) * GATHER // 16]
+            ps = keep.tile([P, GATHER], U8, name=f"picked_scales{n}", align_bytes=64)
+            nc.vector.tensor_copy(ps[:], table_scales[:].indirect(lst))
+            picked_scales.append(ps)
+        for n in range(S // GATHER):
+            lst = offsets[:, n * GATHER // 16 : (n + 1) * GATHER // 16]
+            pw = keep.tile([P, GATHER], I32, name=f"picked_words{n}", align_bytes=64)
+            nc.vector.tensor_copy(pw[:].bitcast(U32), table_words[:].bitcast(U32).indirect(lst))
+            picked_words.append(pw)
+            pt = keep.tile([P, GATHER], F32, name=f"picked_ts{n}")
+            nc.vector.tensor_copy(pt[:], ts_all[:].indirect(lst))
+            picked_ts.append(pt)
+
+        u_grouped = keep.tile([P, M, PACK], BF16, name="u_grouped", align_bytes=64)
+        interleave(nc, u_grouped[:], u_raw[:])
+        u_codes = keep.tile([P, M], U32, name="u_codes", align_bytes=64)
+        u_plane = keep.tile([P, M], U8, name="u_plane", align_bytes=64)
+        nc.vector.quantize_mx(out=u_codes[:].bitcast(FP8X4), scales=u_plane[:], in_=u_grouped[:].rearrange("p n t -> p (n t)"))
+
+        chunks = S // CHUNK
+        c_codes = []
+        c_planes = []
+        for q in range(chunks):
+            grouped = keep.tile([P, CHUNK, PACK], BF16, name=f"c_grouped{q}", tag=f"stage{q}", align_bytes=64)
+            interleave(nc, grouped[:], c_raw[q])
+            codes = keep.tile([P, CHUNK], U32, name=f"c_codes{q}", align_bytes=64)
+            plane = keep.tile([P, CHUNK], U8, name=f"c_plane{q}", align_bytes=64)
+            nc.vector.quantize_mx(out=codes[:].bitcast(FP8X4), scales=plane[:], in_=grouped[:].rearrange("p j t -> p (j t)"))
+            c_codes.append(codes)
+            c_planes.append(plane)
+
+        out_rows = out.rearrange("(h p) j -> p h j", p=P)
+        for q in range(chunks):
+            n, j0 = divmod(q * CHUNK, GATHER)
+            acc = psum.tile([P, HALVES, CHUNK], F32, name=f"acc{q}")
+            for h in range(HALVES):
+                for s0 in range(0, CHUNK, P):
+                    cols = slice(j0 + s0, j0 + s0 + P)
+                    nc.tensor.matmul_mx(
+                        out=acc[:, h, s0 : s0 + P],
+                        lhsT=w4_codes[:, 2 * P * h : 2 * P * (h + 1)].bitcast(FP4X4),
+                        lhsT_scale=w4_plane[:, P * h : P * (h + 1)],
+                        rhs=picked_words[n][:, cols].bitcast(FP8X4),
+                        rhs_scale=picked_scales[n][:, cols],
+                        start=(h == 0 and s0 == 0),
+                        stop=False,
+                    )
+            for h in range(HALVES):
+                nc.tensor.matmul_mx(
+                    out=acc[:, h, :],
+                    lhsT=u_codes[:, P * h : P * (h + 1)].bitcast(FP8X4),
+                    lhsT_scale=u_plane[:, P * h : P * (h + 1)],
+                    rhs=c_codes[q][:].bitcast(FP8X4),
+                    rhs_scale=c_planes[q][:],
+                    start=False,
+                    stop=(h == HALVES - 1),
+                )
+            scaled = keep.tile([P, HALVES, CHUNK], F32, name=f"scaled{q}", tag=f"stage{(q + 2) % chunks}", align_bytes=64)
+            factor = picked_ts[n][:, j0 : j0 + CHUNK].unsqueeze(1).to_broadcast([P, HALVES, CHUNK])
+            nc.vector.tensor_tensor(scaled[:], acc[:], factor, MULT)
+            top = PACK * S - q * HALVES * CHUNK
+            result = raw[:, top - HALVES * CHUNK : top].rearrange("p (h j) -> p h j", h=HALVES)
+            for h in range(HALVES):
+                nc.scalar.activation(result[:, h, :], scaled[:, h, :], IDENT, bias=bias[:, h : h + 1])
+            nc.sync.dma_start(out=out_rows[:, :, q * CHUNK : (q + 1) * CHUNK], in_=result)

@@ -20,8 +20,7 @@ P = 128
 PACK = 4
 HALVES = M // P
 CHUNK = 256
-C_LOADS = (256, 256, 256, 256)
-GATHER = 512
+EARLY = 1
 TS_ROW = T // P
 BANK = 512
 
@@ -48,7 +47,7 @@ def tile_list_tabts_bias_kernel(tc, tab_words, tab_scales, w4_words, w4_scales, 
         offsets = keep.tile([P, S // 16], U16, name="offsets")
         nc.sync.dma_start(offsets[:], offs)
 
-        ts_rows = keep.tile([P, TS_ROW], F32, name="ts_rows")
+        ts_rows = late.tile([P, TS_ROW], F32, name="ts_rows", offset=4 * T + 3 * M + 4 * PACK * EARLY * CHUNK)
         nc.sync.dma_start(out=ts_rows[:], in_=ts[0].rearrange("(p i) -> p i", i=TS_ROW))
 
         u_raw = keep.tile([P, PACK, M], F32, name="u_raw")
@@ -58,38 +57,37 @@ def tile_list_tabts_bias_kernel(tc, tab_words, tab_scales, w4_words, w4_scales, 
         nc.gpsimd.memset(table_scales[:].bitcast(I32), 0)
         load_scale_rows((nc.sync, nc.scalar), table_scales, tab_scales[0])
 
-        zeros = late.tile([P, P], F32, name="zeros", offset=4 * T - 256)
-        nc.gpsimd.memset(zeros[:], 0.0)
+        scratch = late.tile([P, 224], F32, name="scratch", offset=4 * T - 64)
+        zeros = scratch[:, 0:P]
+        nc.vector.memset(zeros, 0.0)
         ident = keep.tile([P, P], F32, name="ident")
         nc.gpsimd.affine_select(
-            out=ident[:], in_=zeros[:], pattern=[[-1, P]], compare_op=mybir.AluOpType.not_equal,
+            out=ident[:], in_=zeros, pattern=[[-1, P]], compare_op=mybir.AluOpType.not_equal,
             fill=1.0, base=0, channel_multiplier=1,
         )
 
         table_words = late.tile([P, T], I32, name="table_words", align_bytes=64, offset=0)
         nc.sync.dma_start(out=table_words[:], in_=tab_words[0].rearrange("p t i -> p (t i)").bitcast(I32))
 
-        raw = late.tile([P, PACK * S + HALVES], F32, name="raw", offset=4 * T)
-        bias = raw[:, PACK * S : PACK * S + HALVES]
-        w4 = keep.tile([P, 3 * M], U8, name="w4", align_bytes=64)
-        w4_codes = w4[:, 0 : 2 * M]
-        w4_plane = w4[:, 2 * M : 3 * M]
-
+        chunks = S // CHUNK
         c_rows = c.rearrange("(p t) j -> p t j", t=PACK)
         c_raw = []
-        start = 0
-        for n, width in enumerate(C_LOADS):
-            if n == len(C_LOADS) - 1:
-                nc.gpsimd.memset(w4[:].bitcast(I32), 0)
-                nc.sync.dma_start(out=w4_codes.bitcast(I32), in_=w4_words[0].bitcast(I32))
-                load_scale_rows((nc.sync,), w4_plane, w4_scales[0])
-            part = raw[:, PACK * start : PACK * (start + width)].rearrange("p (t j) -> p t j", t=PACK)
-            nc.sync.dma_start(out=part, in_=c_rows[:, :, start : start + width])
-            for j0 in range(0, width, CHUNK):
-                c_raw.append(part[:, :, j0 : j0 + CHUNK])
-            start = start + width
-        with nc.allow_non_contiguous_dma(reason="one bias value for each partition"):
-            nc.sync.dma_start(out=bias, in_=b.rearrange("(h p) -> p h", p=P))
+
+        def load_c(tile, q):
+            n = q if q < EARLY else q - EARLY
+            part = tile[:, PACK * CHUNK * n : PACK * CHUNK * (n + 1)].rearrange("p (t j) -> p t j", t=PACK)
+            nc.sync.dma_start(out=part, in_=c_rows[:, :, q * CHUNK : (q + 1) * CHUNK])
+            c_raw.append(part)
+
+        raw_early = late.tile([P, PACK * EARLY * CHUNK], F32, name="raw_early", offset=4 * T + 3 * M)
+        load_c(raw_early, 0)
+
+        w4 = late.tile([P, 3 * M], U8, name="w4", align_bytes=64, offset=4 * T)
+        w4_codes = w4[:, 0 : 2 * M]
+        w4_plane = w4[:, 2 * M : 3 * M]
+        nc.gpsimd.memset(w4[:].bitcast(I32), 0)
+        nc.sync.dma_start(out=w4_codes.bitcast(I32), in_=w4_words[0].bitcast(I32))
+        load_scale_rows((nc.sync,), w4_plane, w4_scales[0])
 
         ts_all = keep.tile([P, T], F32, name="ts_all")
         ts_groups = ts_all[:].rearrange("m (p g i) -> m g p i", g=4, i=4)
@@ -100,22 +98,24 @@ def tile_list_tabts_bias_kernel(tc, tab_words, tab_scales, w4_words, w4_scales, 
                 nc.tensor.transpose(spread[:, i, :], ts_rows[:, col : col + 1].to_broadcast([P, P]), ident[:])
             nc.scalar.copy(out=ts_groups[:, g], in_=spread[:].rearrange("m i p -> m p i"))
 
-        picked_scales = []
+        late_words = PACK * (chunks - EARLY) * CHUNK
+        raw_late = late.tile([P, late_words + HALVES], F32, name="raw_late", offset=4 * T + 3 * M + 4 * PACK * EARLY * CHUNK)
+        for q in range(EARLY, chunks):
+            load_c(raw_late, q)
+        bias = raw_late[:, late_words : late_words + HALVES]
+        with nc.allow_non_contiguous_dma(reason="one bias value for each partition"):
+            nc.sync.dma_start(out=bias, in_=b.rearrange("(h p) -> p h", p=P))
+
+        picked_scales = keep.tile([P, S], U8, name="picked_scales", align_bytes=64)
+        nc.vector.tensor_copy(picked_scales[:], table_scales[:].indirect(offsets[:]))
         picked_words = []
-        picked_ts = []
-        for n in range(S // GATHER):
-            lst = offsets[:, n * GATHER // 16 : (n + 1) * GATHER // 16]
-            ps = keep.tile([P, GATHER], U8, name=f"picked_scales{n}", align_bytes=64)
-            nc.vector.tensor_copy(ps[:], table_scales[:].indirect(lst))
-            picked_scales.append(ps)
-        for n in range(S // GATHER):
-            lst = offsets[:, n * GATHER // 16 : (n + 1) * GATHER // 16]
-            pw = keep.tile([P, GATHER], I32, name=f"picked_words{n}", align_bytes=64)
-            nc.vector.tensor_copy(pw[:].bitcast(U32), table_words[:].bitcast(U32).indirect(lst))
-            picked_words.append(pw)
-            pt = keep.tile([P, GATHER], F32, name=f"picked_ts{n}")
-            nc.vector.tensor_copy(pt[:], ts_all[:].indirect(lst))
-            picked_ts.append(pt)
+        for n in range(S // BANK):
+            words = keep.tile([P, BANK], I32, name=f"picked_words{n}", align_bytes=64)
+            part = offsets[:, n * BANK // 16 : (n + 1) * BANK // 16]
+            nc.vector.tensor_copy(words[:].bitcast(U32), table_words[:].bitcast(U32).indirect(part))
+            picked_words.append(words)
+        picked_ts = late.tile([P, S], F32, name="picked_ts", offset=0)
+        nc.vector.tensor_copy(picked_ts[:], ts_all[:].indirect(offsets[:]))
 
         u_grouped = keep.tile([P, M, PACK], BF16, name="u_grouped", align_bytes=64)
         interleave(nc, u_grouped[:], u_raw[:])
@@ -123,7 +123,6 @@ def tile_list_tabts_bias_kernel(tc, tab_words, tab_scales, w4_words, w4_scales, 
         u_plane = keep.tile([P, M], U8, name="u_plane", align_bytes=64)
         nc.vector.quantize_mx(out=u_codes[:].bitcast(FP8X4), scales=u_plane[:], in_=u_grouped[:].rearrange("p n t -> p (n t)"))
 
-        chunks = S // CHUNK
         c_codes = []
         c_planes = []
         for q in range(chunks):
@@ -135,37 +134,45 @@ def tile_list_tabts_bias_kernel(tc, tab_words, tab_scales, w4_words, w4_scales, 
             c_codes.append(codes)
             c_planes.append(plane)
 
-        out_rows = out.rearrange("(h p) j -> p h j", p=P)
-        for q in range(chunks):
-            n, j0 = divmod(q * CHUNK, GATHER)
-            acc = psum.tile([P, HALVES, CHUNK], F32, name=f"acc{q}")
+
+        sums = []
+        for n in range(S // BANK):
             for h in range(HALVES):
-                for s0 in range(0, CHUNK, P):
-                    cols = slice(j0 + s0, j0 + s0 + P)
-                    nc.tensor.matmul_mx(
-                        out=acc[:, h, s0 : s0 + P],
-                        lhsT=w4_codes[:, 2 * P * h : 2 * P * (h + 1)].bitcast(FP4X4),
-                        lhsT_scale=w4_plane[:, P * h : P * (h + 1)],
-                        rhs=picked_words[n][:, cols].bitcast(FP8X4),
-                        rhs_scale=picked_scales[n][:, cols],
-                        start=(h == 0 and s0 == 0),
-                        stop=False,
-                    )
+                acc = psum.tile([P, BANK], F32, name=f"acc{n}{h}")
+                nc.tensor.matmul_mx(
+                    out=acc[:],
+                    lhsT=w4_codes[:, 2 * P * h : 2 * P * (h + 1)].bitcast(FP4X4),
+                    lhsT_scale=w4_plane[:, P * h : P * (h + 1)],
+                    rhs=picked_words[n][:].bitcast(FP8X4),
+                    rhs_scale=picked_scales[:, n * BANK : (n + 1) * BANK],
+                    start=True,
+                    stop=False,
+                )
+                sums.append(acc)
+
+        for q in range(chunks):
+            n, j0 = divmod(q * CHUNK, BANK)
             for h in range(HALVES):
                 nc.tensor.matmul_mx(
-                    out=acc[:, h, :],
+                    out=sums[n * HALVES + h][:, j0 : j0 + CHUNK],
                     lhsT=u_codes[:, P * h : P * (h + 1)].bitcast(FP8X4),
                     lhsT_scale=u_plane[:, P * h : P * (h + 1)],
                     rhs=c_codes[q][:].bitcast(FP8X4),
                     rhs_scale=c_planes[q][:],
                     start=False,
-                    stop=(h == HALVES - 1),
+                    stop=(j0 + CHUNK == BANK),
                 )
-            scaled = keep.tile([P, HALVES, CHUNK], F32, name=f"scaled{q}", tag=f"stage{(q + 2) % chunks}", align_bytes=64)
-            factor = picked_ts[n][:, j0 : j0 + CHUNK].unsqueeze(1).to_broadcast([P, HALVES, CHUNK])
-            nc.vector.tensor_tensor(scaled[:], acc[:], factor, MULT)
-            top = PACK * S - q * HALVES * CHUNK
-            result = raw[:, top - HALVES * CHUNK : top].rearrange("p (h j) -> p h j", h=HALVES)
-            for h in range(HALVES):
-                nc.scalar.activation(result[:, h, :], scaled[:, h, :], IDENT, bias=bias[:, h : h + 1])
-            nc.sync.dma_start(out=out_rows[:, :, q * CHUNK : (q + 1) * CHUNK], in_=result)
+
+        for bank, acc in enumerate(sums):
+            n, h = divmod(bank, HALVES)
+            scaled = keep.tile([P, BANK], F32, name=f"scaled{bank}", tag=f"stage{(bank + 2) % chunks}", align_bytes=64)
+            result = raw_late[:, late_words - (bank + 1) * BANK : late_words - bank * BANK]
+            last = bank == len(sums) - 1
+            width = CHUNK if last else BANK
+            for j0 in range(0, BANK, width):
+                here = slice(j0, j0 + width)
+                cols = slice(n * BANK + j0, n * BANK + j0 + width)
+                nc.vector.tensor_tensor(scaled[:, here], acc[:, here], picked_ts[:, cols], MULT)
+                nc.scalar.activation(result[:, here], scaled[:, here], IDENT, bias=bias[:, h : h + 1])
+                queue = nc.scalar if last and j0 + width == BANK else nc.sync
+                queue.dma_start(out=out[h * P : (h + 1) * P, cols], in_=result[:, here])

@@ -32,8 +32,8 @@ def load_scale_rows(queues, plane, rows):
 
 def interleave(nc, grouped, raw):
     nc.scalar.copy(
-        out=grouped.rearrange("p (c i) t -> p c t i", i=4),
-        in_=raw.rearrange("p t (c i) -> p c t i", i=4),
+        out=grouped.rearrange("p (c i) t -> p c t i", i=2),
+        in_=raw.rearrange("p t (c i) -> p c t i", i=2),
     )
 
 

@@ -14,13 +14,13 @@ U8 = mybir.dt.uint8
 FP8X4 = mybir.dt.float8_e4m3fn_x4
 FP4X4 = mybir.dt.float4_e2m1fn_x4
 MULT = mybir.AluOpType.mult
+ADD = mybir.AluOpType.add
 IDENT = mybir.ActivationFunctionType.Identity
 
 P = 128
 PACK = 4
 HALVES = M // P
 CHUNK = 256
-EARLY = 1
 TS_ROW = T // P
 BANK = 512
 
@@ -39,6 +39,7 @@ def interleave(nc, grouped, raw):
 
 def tile_list_tabts_bias_kernel(tc, tab_words, tab_scales, w4_words, w4_scales, c, u, ts, b, offs, out):
     nc = tc.nc
+    chunks = S // CHUNK
     with ExitStack() as ctx:
         keep = ctx.enter_context(tc.tile_pool(name="keep", bufs=1))
         late = ctx.enter_context(tc.tile_pool(name="late", bufs=1))
@@ -46,12 +47,13 @@ def tile_list_tabts_bias_kernel(tc, tab_words, tab_scales, w4_words, w4_scales, 
 
         offsets = keep.tile([P, S // 16], U16, name="offsets")
         nc.sync.dma_start(offsets[:], offs)
-
-        ts_rows = late.tile([P, TS_ROW], F32, name="ts_rows", offset=4 * T + 3 * M + 4 * PACK * EARLY * CHUNK)
+        early_at = 4 * T + 3 * M
+        early_words = PACK * (M + CHUNK)
+        rest_at = early_at + 4 * early_words
+        rest_words = PACK * (S - CHUNK)
+        grouped_at = rest_at + 4 * rest_words + 64
+        ts_rows = late.tile([P, TS_ROW], F32, name="ts_rows", offset=rest_at)
         nc.sync.dma_start(out=ts_rows[:], in_=ts[0].rearrange("(p i) -> p i", i=TS_ROW))
-
-        u_raw = keep.tile([P, PACK, M], F32, name="u_raw")
-        nc.sync.dma_start(out=u_raw[:], in_=u.rearrange("(p t) n -> p t n", t=PACK))
 
         table_scales = keep.tile([P, T], U8, name="table_scales", align_bytes=64)
         nc.gpsimd.memset(table_scales[:].bitcast(I32), 0)
@@ -59,7 +61,7 @@ def tile_list_tabts_bias_kernel(tc, tab_words, tab_scales, w4_words, w4_scales, 
 
         scratch = late.tile([P, 224], F32, name="scratch", offset=4 * T - 64)
         zeros = scratch[:, 0:P]
-        nc.vector.memset(zeros, 0.0)
+        nc.gpsimd.memset(zeros, 0.0)
         ident = keep.tile([P, P], F32, name="ident")
         nc.gpsimd.affine_select(
             out=ident[:], in_=zeros, pattern=[[-1, P]], compare_op=mybir.AluOpType.not_equal,
@@ -69,19 +71,20 @@ def tile_list_tabts_bias_kernel(tc, tab_words, tab_scales, w4_words, w4_scales, 
         table_words = late.tile([P, T], I32, name="table_words", align_bytes=64, offset=0)
         nc.sync.dma_start(out=table_words[:], in_=tab_words[0].rearrange("p t i -> p (t i)").bitcast(I32))
 
-        chunks = S // CHUNK
+        early = late.tile([P, early_words], F32, name="early", offset=early_at)
+        u_raw = early[:, 0 : PACK * M].rearrange("p (t n) -> p t n", t=PACK)
+        nc.sync.dma_start(out=u_raw, in_=u.rearrange("(p t) n -> p t n", t=PACK))
+
         c_rows = c.rearrange("(p t) j -> p t j", t=PACK)
         c_raw = []
 
-        def load_c(tile, q):
-            n = q if q < EARLY else q - EARLY
-            part = tile[:, PACK * CHUNK * n : PACK * CHUNK * (n + 1)].rearrange("p (t j) -> p t j", t=PACK)
+        def load_c(tile, at):
+            q = len(c_raw)
+            part = tile[:, at : at + PACK * CHUNK].rearrange("p (t j) -> p t j", t=PACK)
             nc.sync.dma_start(out=part, in_=c_rows[:, :, q * CHUNK : (q + 1) * CHUNK])
             c_raw.append(part)
 
-        raw_early = late.tile([P, PACK * EARLY * CHUNK], F32, name="raw_early", offset=4 * T + 3 * M)
-        load_c(raw_early, 0)
-
+        load_c(early, PACK * M)
         w4 = late.tile([P, 3 * M], U8, name="w4", align_bytes=64, offset=4 * T)
         w4_codes = w4[:, 0 : 2 * M]
         w4_plane = w4[:, 2 * M : 3 * M]
@@ -92,33 +95,28 @@ def tile_list_tabts_bias_kernel(tc, tab_words, tab_scales, w4_words, w4_scales, 
         ts_all = keep.tile([P, T], F32, name="ts_all")
         ts_groups = ts_all[:].rearrange("m (p g i) -> m g p i", g=4, i=4)
         for g in range(4):
-            spread = psum.tile([P, 4, P], F32, name=f"spread{g}")
+            spread = psum.tile([P, 4, P], F32, name=f"spread{g}", tag=f"bank{g}")
             for i in range(4):
                 col = 4 * g + i
                 nc.tensor.transpose(spread[:, i, :], ts_rows[:, col : col + 1].to_broadcast([P, P]), ident[:])
             nc.scalar.copy(out=ts_groups[:, g], in_=spread[:].rearrange("m i p -> m p i"))
 
-        late_words = PACK * (chunks - EARLY) * CHUNK
-        raw_late = late.tile([P, late_words + HALVES], F32, name="raw_late", offset=4 * T + 3 * M + 4 * PACK * EARLY * CHUNK)
-        for q in range(EARLY, chunks):
-            load_c(raw_late, q)
-        bias = raw_late[:, late_words : late_words + HALVES]
+        rest = late.tile([P, rest_words + HALVES], F32, name="rest", offset=rest_at)
+        for q in range(1, chunks):
+            load_c(rest, PACK * CHUNK * (q - 1))
+        bias = rest[:, rest_words : rest_words + HALVES]
         with nc.allow_non_contiguous_dma(reason="one bias value for each partition"):
             nc.sync.dma_start(out=bias, in_=b.rearrange("(h p) -> p h", p=P))
 
         picked_scales = keep.tile([P, S], U8, name="picked_scales", align_bytes=64)
         nc.vector.tensor_copy(picked_scales[:], table_scales[:].indirect(offsets[:]))
-        picked_words = []
-        for n in range(S // BANK):
-            words = keep.tile([P, BANK], I32, name=f"picked_words{n}", align_bytes=64)
-            part = offsets[:, n * BANK // 16 : (n + 1) * BANK // 16]
-            nc.vector.tensor_copy(words[:].bitcast(U32), table_words[:].bitcast(U32).indirect(part))
-            picked_words.append(words)
+        picked_words = keep.tile([P, S], I32, name="picked_words", align_bytes=64)
+        nc.vector.tensor_copy(picked_words[:].bitcast(U32), table_words[:].bitcast(U32).indirect(offsets[:]))
         picked_ts = late.tile([P, S], F32, name="picked_ts", offset=0)
         nc.vector.tensor_copy(picked_ts[:], ts_all[:].indirect(offsets[:]))
 
         u_grouped = keep.tile([P, M, PACK], BF16, name="u_grouped", align_bytes=64)
-        interleave(nc, u_grouped[:], u_raw[:])
+        interleave(nc, u_grouped[:], u_raw)
         u_codes = keep.tile([P, M], U32, name="u_codes", align_bytes=64)
         u_plane = keep.tile([P, M], U8, name="u_plane", align_bytes=64)
         nc.vector.quantize_mx(out=u_codes[:].bitcast(FP8X4), scales=u_plane[:], in_=u_grouped[:].rearrange("p n t -> p (n t)"))
@@ -126,7 +124,7 @@ def tile_list_tabts_bias_kernel(tc, tab_words, tab_scales, w4_words, w4_scales, 
         c_codes = []
         c_planes = []
         for q in range(chunks):
-            grouped = keep.tile([P, CHUNK, PACK], BF16, name=f"c_grouped{q}", tag=f"stage{q}", align_bytes=64)
+            grouped = late.tile([P, CHUNK, PACK], BF16, name=f"c_grouped{q}", align_bytes=64, offset=grouped_at + 2 * PACK * CHUNK * q)
             interleave(nc, grouped[:], c_raw[q])
             codes = keep.tile([P, CHUNK], U32, name=f"c_codes{q}", align_bytes=64)
             plane = keep.tile([P, CHUNK], U8, name=f"c_plane{q}", align_bytes=64)
@@ -134,45 +132,48 @@ def tile_list_tabts_bias_kernel(tc, tab_words, tab_scales, w4_words, w4_scales, 
             c_codes.append(codes)
             c_planes.append(plane)
 
-
+        parts = (
+            (0, BANK, 4, 1, PACK * 2 * CHUNK),
+            (BANK, CHUNK, 6, 3, 0),
+            (BANK + CHUNK, CHUNK, 0, 0, HALVES * CHUNK),
+        )
         sums = []
-        for n in range(S // BANK):
+        for j0, width, bank, over, at in parts:
+            step = BANK if width == BANK else P
             for h in range(HALVES):
-                acc = psum.tile([P, BANK], F32, name=f"acc{n}{h}")
-                nc.tensor.matmul_mx(
-                    out=acc[:],
-                    lhsT=w4_codes[:, 2 * P * h : 2 * P * (h + 1)].bitcast(FP4X4),
-                    lhsT_scale=w4_plane[:, P * h : P * (h + 1)],
-                    rhs=picked_words[n][:].bitcast(FP8X4),
-                    rhs_scale=picked_scales[:, n * BANK : (n + 1) * BANK],
-                    start=True,
-                    stop=False,
-                )
+                acc = psum.tile([P, width], F32, name=f"acc{bank + h}", tag=f"bank{bank + h}")
+                for k0 in range(0, width, step):
+                    nc.tensor.matmul_mx(
+                        out=acc[:, k0 : k0 + step],
+                        lhsT=w4_codes[:, 2 * P * h : 2 * P * (h + 1)].bitcast(FP4X4),
+                        lhsT_scale=w4_plane[:, P * h : P * (h + 1)],
+                        rhs=picked_words[:, j0 + k0 : j0 + k0 + step].bitcast(FP8X4),
+                        rhs_scale=picked_scales[:, j0 + k0 : j0 + k0 + step],
+                        start=(k0 == 0),
+                        stop=False,
+                    )
                 sums.append(acc)
 
-        for q in range(chunks):
-            n, j0 = divmod(q * CHUNK, BANK)
-            for h in range(HALVES):
-                nc.tensor.matmul_mx(
-                    out=sums[n * HALVES + h][:, j0 : j0 + CHUNK],
-                    lhsT=u_codes[:, P * h : P * (h + 1)].bitcast(FP8X4),
-                    lhsT_scale=u_plane[:, P * h : P * (h + 1)],
-                    rhs=c_codes[q][:].bitcast(FP8X4),
-                    rhs_scale=c_planes[q][:],
-                    start=False,
-                    stop=(j0 + CHUNK == BANK),
-                )
+        for n, (j0, width, bank, over, at) in enumerate(parts):
+            for k0 in range(0, width, CHUNK):
+                q = (j0 + k0) // CHUNK
+                for h in range(HALVES):
+                    nc.tensor.matmul_mx(
+                        out=sums[n * HALVES + h][:, k0 : k0 + CHUNK],
+                        lhsT=u_codes[:, P * h : P * (h + 1)].bitcast(FP8X4),
+                        lhsT_scale=u_plane[:, P * h : P * (h + 1)],
+                        rhs=c_codes[q][:].bitcast(FP8X4),
+                        rhs_scale=c_planes[q][:],
+                        start=False,
+                        stop=(k0 + CHUNK == width),
+                    )
 
-        for bank, acc in enumerate(sums):
-            n, h = divmod(bank, HALVES)
-            scaled = keep.tile([P, BANK], F32, name=f"scaled{bank}", tag=f"stage{(bank + 2) % chunks}", align_bytes=64)
-            result = raw_late[:, late_words - (bank + 1) * BANK : late_words - bank * BANK]
-            last = bank == len(sums) - 1
-            width = CHUNK if last else BANK
-            for j0 in range(0, BANK, width):
-                here = slice(j0, j0 + width)
-                cols = slice(n * BANK + j0, n * BANK + j0 + width)
-                nc.vector.tensor_tensor(scaled[:, here], acc[:, here], picked_ts[:, cols], MULT)
-                nc.scalar.activation(result[:, here], scaled[:, here], IDENT, bias=bias[:, h : h + 1])
-                queue = nc.scalar if last and j0 + width == BANK else nc.sync
-                queue.dma_start(out=out[h * P : (h + 1) * P, cols], in_=result[:, here])
+        for n, (j0, width, bank, over, at) in enumerate(parts):
+            scaled = late.tile([P, HALVES, width], F32, name=f"scaled{n}", align_bytes=64, offset=grouped_at + 2 * PACK * CHUNK * over)
+            cols = slice(j0, j0 + width)
+            for h in range(HALVES):
+                result = rest[:, at + h * width : at + (h + 1) * width]
+                nc.vector.tensor_tensor(scaled[:, h, :], sums[n * HALVES + h][:], picked_ts[:, cols], MULT)
+                nc.scalar.activation(result, scaled[:, h, :], IDENT, bias=bias[:, h : h + 1])
+                queue = nc.scalar if n == len(parts) - 1 and h == HALVES - 1 else nc.sync
+                queue.dma_start(out=out[h * P : (h + 1) * P, cols], in_=result)

@@ -133,7 +133,7 @@ def tile_list_tabts_bias_kernel(tc, tab_words, tab_scales, w4_words, w4_scales, 
             c_planes.append(plane)
 
         parts = (
-            (0, BANK, 4, 1, PACK * 2 * CHUNK),
+            (0, BANK, 4, 1, PACK * CHUNK),
             (BANK, CHUNK, 6, 3, 0),
             (BANK + CHUNK, CHUNK, 0, 0, HALVES * CHUNK),
         )
@@ -174,6 +174,9 @@ def tile_list_tabts_bias_kernel(tc, tab_words, tab_scales, w4_words, w4_scales, 
             for h in range(HALVES):
                 result = rest[:, at + h * width : at + (h + 1) * width]
                 nc.vector.tensor_tensor(scaled[:, h, :], sums[n * HALVES + h][:], picked_ts[:, cols], MULT)
-                nc.scalar.activation(result, scaled[:, h, :], IDENT, bias=bias[:, h : h + 1])
+                if n == 0:
+                    nc.gpsimd.tensor_scalar(result, scaled[:, h, :], 1.0, bias[:, h : h + 1], MULT, ADD)
+                else:
+                    nc.scalar.activation(result, scaled[:, h, :], IDENT, bias=bias[:, h : h + 1])
                 queue = nc.scalar if n == len(parts) - 1 and h == HALVES - 1 else nc.sync
                 queue.dma_start(out=out[h * P : (h + 1) * P, cols], in_=result)

@@ -30,8 +30,8 @@ def load_scale_rows(queues, plane, rows):
         queues[q % len(queues)].dma_start(out=plane[32 * q : 32 * q + 4, :].bitcast(I32), in_=rows[4 * q : 4 * q + 4, :].bitcast(I32))
 
 
-def interleave(nc, grouped, raw):
-    nc.scalar.copy(
+def interleave(copy, grouped, raw):
+    copy(
         out=grouped.rearrange("p (c i) t -> p c t i", i=2),
         in_=raw.rearrange("p t (c i) -> p c t i", i=2),
     )
@@ -112,11 +112,18 @@ def tile_list_tabts_bias_kernel(tc, tab_words, tab_scales, w4_words, w4_scales, 
         nc.vector.tensor_copy(picked_scales[:], table_scales[:].indirect(offsets[:]))
         picked_words = keep.tile([P, S], I32, name="picked_words", align_bytes=64)
         nc.vector.tensor_copy(picked_words[:].bitcast(U32), table_words[:].bitcast(U32).indirect(offsets[:]))
-        picked_ts = late.tile([P, S], F32, name="picked_ts", offset=0)
-        nc.vector.tensor_copy(picked_ts[:], ts_all[:].indirect(offsets[:]))
+        picked_ts = []
+
+        def pick_ts(j0, width, at):
+            picked = late.tile([P, width], F32, name=f"picked_ts{j0}", offset=at)
+            nc.vector.tensor_copy(picked[:], ts_all[:].indirect(offsets[:, j0 // 16 : (j0 + width) // 16]))
+            for k0 in range(0, width, CHUNK):
+                picked_ts.append(picked[:, k0 : k0 + CHUNK])
+
+        pick_ts(0, BANK, 0)
 
         u_grouped = keep.tile([P, M, PACK], BF16, name="u_grouped", align_bytes=64)
-        interleave(nc, u_grouped[:], u_raw)
+        interleave(nc.scalar.copy, u_grouped[:], u_raw)
         u_codes = keep.tile([P, M], U32, name="u_codes", align_bytes=64)
         u_plane = keep.tile([P, M], U8, name="u_plane", align_bytes=64)
         nc.vector.quantize_mx(out=u_codes[:].bitcast(FP8X4), scales=u_plane[:], in_=u_grouped[:].rearrange("p n t -> p (n t)"))
@@ -125,58 +132,60 @@ def tile_list_tabts_bias_kernel(tc, tab_words, tab_scales, w4_words, w4_scales, 
         c_planes = []
         for q in range(chunks):
             grouped = late.tile([P, CHUNK, PACK], BF16, name=f"c_grouped{q}", align_bytes=64, offset=grouped_at + 2 * PACK * CHUNK * q)
-            interleave(nc, grouped[:], c_raw[q])
+            interleave(nc.vector.tensor_copy if q == chunks - 1 else nc.scalar.copy, grouped[:], c_raw[q])
             codes = keep.tile([P, CHUNK], U32, name=f"c_codes{q}", align_bytes=64)
             plane = keep.tile([P, CHUNK], U8, name=f"c_plane{q}", align_bytes=64)
             nc.vector.quantize_mx(out=codes[:].bitcast(FP8X4), scales=plane[:], in_=grouped[:].rearrange("p j t -> p (j t)"))
             c_codes.append(codes)
             c_planes.append(plane)
 
-        parts = (
-            (0, BANK, 4, 1, PACK * CHUNK),
-            (BANK, CHUNK, 6, 3, 0),
-            (BANK + CHUNK, CHUNK, 0, 0, HALVES * CHUNK),
-        )
+        pick_ts(2 * CHUNK, CHUNK, grouped_at)
+        pick_ts(3 * CHUNK, CHUNK, grouped_at + 2 * PACK * CHUNK)
+
+        scaled_at = (4 * BANK, 8 * BANK, grouped_at + 2 * PACK * CHUNK * 3, 12 * BANK)
+        result_at = (PACK * CHUNK, PACK * CHUNK + BANK, 0, BANK)
         sums = []
-        for j0, width, bank, over, at in parts:
-            step = BANK if width == BANK else P
+
+        def table_passes(q):
             for h in range(HALVES):
-                acc = psum.tile([P, width], F32, name=f"acc{bank + h}", tag=f"bank{bank + h}")
-                for k0 in range(0, width, step):
+                acc = psum.tile([P, CHUNK], F32, name=f"acc{q}{h}", tag=f"bank{4 + 2 * (q % 2) + h}")
+                for k0 in range(0, CHUNK, P):
+                    cols = slice(q * CHUNK + k0, q * CHUNK + k0 + P)
                     nc.tensor.matmul_mx(
-                        out=acc[:, k0 : k0 + step],
+                        out=acc[:, k0 : k0 + P],
                         lhsT=w4_codes[:, 2 * P * h : 2 * P * (h + 1)].bitcast(FP4X4),
                         lhsT_scale=w4_plane[:, P * h : P * (h + 1)],
-                        rhs=picked_words[:, j0 + k0 : j0 + k0 + step].bitcast(FP8X4),
-                        rhs_scale=picked_scales[:, j0 + k0 : j0 + k0 + step],
+                        rhs=picked_words[:, cols].bitcast(FP8X4),
+                        rhs_scale=picked_scales[:, cols],
                         start=(k0 == 0),
                         stop=False,
                     )
                 sums.append(acc)
 
-        for n, (j0, width, bank, over, at) in enumerate(parts):
-            for k0 in range(0, width, CHUNK):
-                q = (j0 + k0) // CHUNK
-                for h in range(HALVES):
-                    nc.tensor.matmul_mx(
-                        out=sums[n * HALVES + h][:, k0 : k0 + CHUNK],
-                        lhsT=u_codes[:, P * h : P * (h + 1)].bitcast(FP8X4),
-                        lhsT_scale=u_plane[:, P * h : P * (h + 1)],
-                        rhs=c_codes[q][:].bitcast(FP8X4),
-                        rhs_scale=c_planes[q][:],
-                        start=False,
-                        stop=(k0 + CHUNK == width),
-                    )
-
-        for n, (j0, width, bank, over, at) in enumerate(parts):
-            scaled = late.tile([P, HALVES, width], F32, name=f"scaled{n}", align_bytes=64, offset=grouped_at + 2 * PACK * CHUNK * over)
-            cols = slice(j0, j0 + width)
+        def finish(q):
             for h in range(HALVES):
-                result = rest[:, at + h * width : at + (h + 1) * width]
-                nc.vector.tensor_tensor(scaled[:, h, :], sums[n * HALVES + h][:], picked_ts[:, cols], MULT)
-                if n == 0:
-                    nc.gpsimd.tensor_scalar(result, scaled[:, h, :], 1.0, bias[:, h : h + 1], MULT, ADD)
-                else:
-                    nc.scalar.activation(result, scaled[:, h, :], IDENT, bias=bias[:, h : h + 1])
-                queue = nc.scalar if n == len(parts) - 1 and h == HALVES - 1 else nc.sync
-                queue.dma_start(out=out[h * P : (h + 1) * P, cols], in_=result)
+                nc.tensor.matmul_mx(
+                    out=sums[q * HALVES + h][:],
+                    lhsT=u_codes[:, P * h : P * (h + 1)].bitcast(FP8X4),
+                    lhsT_scale=u_plane[:, P * h : P * (h + 1)],
+                    rhs=c_codes[q][:].bitcast(FP8X4),
+                    rhs_scale=c_planes[q][:],
+                    start=False,
+                    stop=True,
+                )
+            scaled = late.tile([P, HALVES, CHUNK], F32, name=f"scaled{q}", align_bytes=64, offset=scaled_at[q])
+            for h in range(HALVES):
+                result = rest[:, result_at[q] + h * CHUNK : result_at[q] + (h + 1) * CHUNK]
+                nc.vector.tensor_tensor(scaled[:, h, :], sums[q * HALVES + h][:], picked_ts[q], MULT)
+                nc.scalar.activation(result, scaled[:, h, :], IDENT, bias=bias[:, h : h + 1])
+                queue = nc.scalar if q == chunks - 1 and h == HALVES - 1 else nc.sync
+                queue.dma_start(out=out[h * P : (h + 1) * P, q * CHUNK : (q + 1) * CHUNK], in_=result)
+
+        table_passes(0)
+        table_passes(1)
+        finish(0)
+        table_passes(2)
+        finish(1)
+        table_passes(3)
+        finish(2)
+        finish(3)

@@ -47,11 +47,11 @@ def tile_list_tabts_bias_kernel(tc, tab_words, tab_scales, w4_words, w4_scales, 
 
         offsets = keep.tile([P, S // 16], U16, name="offsets")
         nc.sync.dma_start(offsets[:], offs)
-        early_at = 4 * T + 3 * M
+        early_at = 4 * T + 3 * M + 32
         early_words = PACK * (M + CHUNK)
         rest_at = early_at + 4 * early_words
         rest_words = PACK * (S - CHUNK)
-        grouped_at = rest_at + 4 * rest_words + 64
+        grouped_at = rest_at + 4 * rest_words + 32
         ts_rows = late.tile([P, TS_ROW], F32, name="ts_rows", offset=rest_at)
         nc.sync.dma_start(out=ts_rows[:], in_=ts[0].rearrange("(p i) -> p i", i=TS_ROW))
 
@@ -91,6 +91,9 @@ def tile_list_tabts_bias_kernel(tc, tab_words, tab_scales, w4_words, w4_scales, 
         nc.gpsimd.memset(w4[:].bitcast(I32), 0)
         nc.sync.dma_start(out=w4_codes.bitcast(I32), in_=w4_words[0].bitcast(I32))
         load_scale_rows((nc.sync,), w4_plane, w4_scales[0])
+        bias = late.tile([P, HALVES], F32, name="bias", offset=4 * T + 3 * M)
+        with nc.allow_non_contiguous_dma(reason="one bias value for each partition"):
+            nc.gpsimd.dma_start(out=bias[:], in_=b.rearrange("(h p) -> p h", p=P))
 
         ts_all = keep.tile([P, T], F32, name="ts_all")
         ts_groups = ts_all[:].rearrange("m (p g i) -> m g p i", g=4, i=4)
@@ -101,12 +104,9 @@ def tile_list_tabts_bias_kernel(tc, tab_words, tab_scales, w4_words, w4_scales, 
                 nc.tensor.transpose(spread[:, i, :], ts_rows[:, col : col + 1].to_broadcast([P, P]), ident[:])
             nc.scalar.copy(out=ts_groups[:, g], in_=spread[:].rearrange("m i p -> m p i"))
 
-        rest = late.tile([P, rest_words + HALVES], F32, name="rest", offset=rest_at)
+        rest = late.tile([P, rest_words], F32, name="rest", offset=rest_at)
         for q in range(1, chunks):
             load_c(rest, PACK * CHUNK * (q - 1))
-        bias = rest[:, rest_words : rest_words + HALVES]
-        with nc.allow_non_contiguous_dma(reason="one bias value for each partition"):
-            nc.sync.dma_start(out=bias, in_=b.rearrange("(h p) -> p h", p=P))
 
         picked_scales = keep.tile([P, S], U8, name="picked_scales", align_bytes=64)
         nc.vector.tensor_copy(picked_scales[:], table_scales[:].indirect(offsets[:]))
@@ -132,7 +132,11 @@ def tile_list_tabts_bias_kernel(tc, tab_words, tab_scales, w4_words, w4_scales, 
         c_planes = []
         for q in range(chunks):
             grouped = late.tile([P, CHUNK, PACK], BF16, name=f"c_grouped{q}", align_bytes=64, offset=grouped_at + 2 * PACK * CHUNK * q)
-            interleave(nc.vector.tensor_copy if q == chunks - 1 else nc.scalar.copy, grouped[:], c_raw[q])
+            if q < chunks - 1:
+                interleave(nc.scalar.copy, grouped[:], c_raw[q])
+            else:
+                interleave(nc.scalar.copy, grouped[:, 0:P, :], c_raw[q][:, :, 0:P])
+                interleave(nc.vector.tensor_copy, grouped[:, P:CHUNK, :], c_raw[q][:, :, P:CHUNK])
             codes = keep.tile([P, CHUNK], U32, name=f"c_codes{q}", align_bytes=64)
             plane = keep.tile([P, CHUNK], U8, name=f"c_plane{q}", align_bytes=64)
             nc.vector.quantize_mx(out=codes[:].bitcast(FP8X4), scales=plane[:], in_=grouped[:].rearrange("p j t -> p (j t)"))
@@ -143,7 +147,7 @@ def tile_list_tabts_bias_kernel(tc, tab_words, tab_scales, w4_words, w4_scales, 
         pick_ts(3 * CHUNK, CHUNK, grouped_at + 2 * PACK * CHUNK)
 
         scaled_at = (4 * BANK, 8 * BANK, grouped_at + 2 * PACK * CHUNK * 3, 12 * BANK)
-        result_at = (PACK * CHUNK, PACK * CHUNK + BANK, 0, BANK)
+        results = keep.tile([P, chunks, CHUNK], F32, name="results")
         sums = []
 
         def table_passes(q):
@@ -175,9 +179,16 @@ def tile_list_tabts_bias_kernel(tc, tab_words, tab_scales, w4_words, w4_scales, 
                 )
             scaled = late.tile([P, HALVES, CHUNK], F32, name=f"scaled{q}", align_bytes=64, offset=scaled_at[q])
             for h in range(HALVES):
-                result = rest[:, result_at[q] + h * CHUNK : result_at[q] + (h + 1) * CHUNK]
                 nc.vector.tensor_tensor(scaled[:, h, :], sums[q * HALVES + h][:], picked_ts[q], MULT)
-                nc.scalar.activation(result, scaled[:, h, :], IDENT, bias=bias[:, h : h + 1])
+                if h == 0 and q == chunks - 1:
+                    result = results[:, q, :]
+                    nc.scalar.activation(result, scaled[:, h, :], IDENT, bias=bias[:, h : h + 1])
+                elif h == 0:
+                    result = results[:, q, :]
+                    nc.gpsimd.tensor_scalar(result, scaled[:, h, :], 1.0, bias[:, h : h + 1], MULT, ADD)
+                else:
+                    result = rest[:, rest_words - (q + 1) * CHUNK : rest_words - q * CHUNK]
+                    nc.scalar.activation(result, scaled[:, h, :], IDENT, bias=bias[:, h : h + 1])
                 queue = nc.scalar if q == chunks - 1 and h == HALVES - 1 else nc.sync
                 queue.dma_start(out=out[h * P : (h + 1) * P, q * CHUNK : (q + 1) * CHUNK], in_=result)
 

@@ -61,7 +61,7 @@ def tile_list_tabts_bias_kernel(tc, tab_words, tab_scales, w4_words, w4_scales, 
 
         scratch = late.tile([P, 224], F32, name="scratch", offset=4 * T - 64)
         zeros = scratch[:, 0:P]
-        nc.gpsimd.memset(zeros, 0.0)
+        nc.vector.memset(zeros, 0.0)
         ident = keep.tile([P, P], F32, name="ident")
         nc.gpsimd.affine_select(
             out=ident[:], in_=zeros, pattern=[[-1, P]], compare_op=mybir.AluOpType.not_equal,
@@ -132,11 +132,7 @@ def tile_list_tabts_bias_kernel(tc, tab_words, tab_scales, w4_words, w4_scales, 
         c_planes = []
         for q in range(chunks):
             grouped = late.tile([P, CHUNK, PACK], BF16, name=f"c_grouped{q}", align_bytes=64, offset=grouped_at + 2 * PACK * CHUNK * q)
-            if q < chunks - 1:
-                interleave(nc.scalar.copy, grouped[:], c_raw[q])
-            else:
-                interleave(nc.scalar.copy, grouped[:, 0:P, :], c_raw[q][:, :, 0:P])
-                interleave(nc.vector.tensor_copy, grouped[:, P:CHUNK, :], c_raw[q][:, :, P:CHUNK])
+            interleave(nc.scalar.copy, grouped[:], c_raw[q])
             codes = keep.tile([P, CHUNK], U32, name=f"c_codes{q}", align_bytes=64)
             plane = keep.tile([P, CHUNK], U8, name=f"c_plane{q}", align_bytes=64)
             nc.vector.quantize_mx(out=codes[:].bitcast(FP8X4), scales=plane[:], in_=grouped[:].rearrange("p j t -> p (j t)"))
@@ -152,7 +148,7 @@ def tile_list_tabts_bias_kernel(tc, tab_words, tab_scales, w4_words, w4_scales, 
 
         def table_passes(q):
             for h in range(HALVES):
-                acc = psum.tile([P, CHUNK], F32, name=f"acc{q}{h}", tag=f"bank{4 + 2 * (q % 2) + h}")
+                acc = psum.tile([P, CHUNK], F32, name=f"acc{q}{h}", tag=f"bank{(4, 6, 0, 4)[q] + h}")
                 for k0 in range(0, CHUNK, P):
                     cols = slice(q * CHUNK + k0, q * CHUNK + k0 + P)
                     nc.tensor.matmul_mx(
@@ -194,9 +190,9 @@ def tile_list_tabts_bias_kernel(tc, tab_words, tab_scales, w4_words, w4_scales, 
 
         table_passes(0)
         table_passes(1)
-        finish(0)
         table_passes(2)
-        finish(1)
+        finish(0)
         table_passes(3)
+        finish(1)
         finish(2)
         finish(3)

@@ -57,7 +57,7 @@ def tile_list_tabts_bias_kernel(tc, tab_words, tab_scales, w4_words, w4_scales, 
 
         table_scales = keep.tile([P, T], U8, name="table_scales", align_bytes=64)
         nc.gpsimd.memset(table_scales[:].bitcast(I32), 0)
-        load_scale_rows((nc.sync, nc.scalar), table_scales, tab_scales[0])
+        load_scale_rows((nc.sync, nc.scalar, nc.scalar, nc.scalar), table_scales, tab_scales[0])
 
         scratch = late.tile([P, 224], F32, name="scratch", offset=4 * T - 64)
         zeros = scratch[:, 0:P]
@@ -175,18 +175,18 @@ def tile_list_tabts_bias_kernel(tc, tab_words, tab_scales, w4_words, w4_scales, 
                 )
             scaled = late.tile([P, HALVES, CHUNK], F32, name=f"scaled{q}", align_bytes=64, offset=scaled_at[q])
             for h in range(HALVES):
-                nc.vector.tensor_tensor(scaled[:, h, :], sums[q * HALVES + h][:], picked_ts[q], MULT)
-                if h == 0 and q == chunks - 1:
-                    result = results[:, q, :]
-                    nc.scalar.activation(result, scaled[:, h, :], IDENT, bias=bias[:, h : h + 1])
-                elif h == 0:
-                    result = results[:, q, :]
-                    nc.gpsimd.tensor_scalar(result, scaled[:, h, :], 1.0, bias[:, h : h + 1], MULT, ADD)
-                else:
-                    result = rest[:, rest_words - (q + 1) * CHUNK : rest_words - q * CHUNK]
-                    nc.scalar.activation(result, scaled[:, h, :], IDENT, bias=bias[:, h : h + 1])
-                queue = nc.scalar if q == chunks - 1 and h == HALVES - 1 else nc.sync
-                queue.dma_start(out=out[h * P : (h + 1) * P, q * CHUNK : (q + 1) * CHUNK], in_=result)
+                result = results[:, q, :] if h == 0 else rest[:, rest_words - (q + 1) * CHUNK : rest_words - q * CHUNK]
+                last = q == chunks - 1 and h == HALVES - 1
+                width = CHUNK // 2 if last else CHUNK
+                for k0 in range(0, CHUNK, width):
+                    here = slice(k0, k0 + width)
+                    nc.vector.tensor_tensor(scaled[:, h, here], sums[q * HALVES + h][:, here], picked_ts[q][:, here], MULT)
+                    if h == 0 and q < chunks - 1:
+                        nc.gpsimd.tensor_scalar(result[:, here], scaled[:, h, here], 1.0, bias[:, h : h + 1], MULT, ADD)
+                    else:
+                        nc.scalar.activation(result[:, here], scaled[:, h, here], IDENT, bias=bias[:, h : h + 1])
+                    queue = nc.scalar if last and k0 > 0 else nc.sync
+                    queue.dma_start(out=out[h * P : (h + 1) * P, q * CHUNK + k0 : q * CHUNK + k0 + width], in_=result[:, here])
 
         table_passes(0)
         table_passes(1)

@@ -21,17 +21,34 @@ P = 128
 PACK = 4
 HALVES = M // P
 CHUNK = 256
+CHUNKS = S // CHUNK
+LAST = CHUNKS - 1
 TS_ROW = T // P
-BANK = 512
+SHARE = 64
+
+WORDS_AT = 0
+W4_AT = WORDS_AT + 4 * T
+BIAS_AT = W4_AT + 3 * M
+EARLY_AT = BIAS_AT + 32
+EARLY_WORDS = PACK * (M + CHUNK)
+REST_AT = EARLY_AT + 4 * EARLY_WORDS
+REST_WORDS = PACK * (S - CHUNK)
+GROUPED_AT = REST_AT + 4 * REST_WORDS + 32
+GROUPED_BYTES = 2 * PACK * CHUNK
+SCALED_BYTES = 4 * HALVES * CHUNK
+GATE_AT = W4_AT - 64
+GATE_WORDS = (EARLY_AT + 32 - GATE_AT) // 4
+
+SUM_BANKS = (4, 6, 0, 4)
 
 
-def load_scale_rows(queues, plane, rows):
+def load_scale_rows(nc, plane, rows):
     for q in range(4):
-        queues[q % len(queues)].dma_start(out=plane[32 * q : 32 * q + 4, :].bitcast(I32), in_=rows[4 * q : 4 * q + 4, :].bitcast(I32))
+        nc.sync.dma_start(out=plane[32 * q : 32 * q + 4, :].bitcast(I32), in_=rows[4 * q : 4 * q + 4, :].bitcast(I32))
 
 
-def interleave(copy, grouped, raw):
-    copy(
+def interleave(nc, grouped, raw):
+    nc.scalar.copy(
         out=grouped.rearrange("p (c i) t -> p c t i", i=2),
         in_=raw.rearrange("p t (c i) -> p c t i", i=2),
     )
@@ -39,28 +56,23 @@ def interleave(copy, grouped, raw):
 
 def tile_list_tabts_bias_kernel(tc, tab_words, tab_scales, w4_words, w4_scales, c, u, ts, b, offs, out):
     nc = tc.nc
-    chunks = S // CHUNK
     with ExitStack() as ctx:
         keep = ctx.enter_context(tc.tile_pool(name="keep", bufs=1))
-        late = ctx.enter_context(tc.tile_pool(name="late", bufs=1))
+        placed = ctx.enter_context(tc.tile_pool(name="placed", bufs=1))
         psum = ctx.enter_context(tc.psum_pool(name="psum", bufs=1))
 
         offsets = keep.tile([P, S // 16], U16, name="offsets")
         nc.sync.dma_start(offsets[:], offs)
-        early_at = 4 * T + 3 * M + 32
-        early_words = PACK * (M + CHUNK)
-        rest_at = early_at + 4 * early_words
-        rest_words = PACK * (S - CHUNK)
-        grouped_at = rest_at + 4 * rest_words + 32
-        ts_rows = late.tile([P, TS_ROW], F32, name="ts_rows", offset=rest_at)
+
+        ts_rows = placed.tile([P, TS_ROW], F32, name="ts_rows", offset=REST_AT)
         nc.sync.dma_start(out=ts_rows[:], in_=ts[0].rearrange("(p i) -> p i", i=TS_ROW))
 
         table_scales = keep.tile([P, T], U8, name="table_scales", align_bytes=64)
         nc.gpsimd.memset(table_scales[:].bitcast(I32), 0)
-        load_scale_rows((nc.sync, nc.scalar, nc.scalar, nc.scalar), table_scales, tab_scales[0])
+        load_scale_rows(nc, table_scales, tab_scales[0])
 
-        scratch = late.tile([P, 224], F32, name="scratch", offset=4 * T - 64)
-        zeros = scratch[:, 0:P]
+        gate = placed.tile([P, GATE_WORDS], F32, name="gate", offset=GATE_AT)
+        zeros = gate[:, 0:P]
         nc.vector.memset(zeros, 0.0)
         ident = keep.tile([P, P], F32, name="ident")
         nc.gpsimd.affine_select(
@@ -68,30 +80,32 @@ def tile_list_tabts_bias_kernel(tc, tab_words, tab_scales, w4_words, w4_scales, 
             fill=1.0, base=0, channel_multiplier=1,
         )
 
-        table_words = late.tile([P, T], I32, name="table_words", align_bytes=64, offset=0)
+        table_words = placed.tile([P, T], I32, name="table_words", align_bytes=64, offset=WORDS_AT)
         nc.sync.dma_start(out=table_words[:], in_=tab_words[0].rearrange("p t i -> p (t i)").bitcast(I32))
 
-        early = late.tile([P, early_words], F32, name="early", offset=early_at)
+        early = placed.tile([P, EARLY_WORDS], F32, name="early", offset=EARLY_AT)
         u_raw = early[:, 0 : PACK * M].rearrange("p (t n) -> p t n", t=PACK)
         nc.sync.dma_start(out=u_raw, in_=u.rearrange("(p t) n -> p t n", t=PACK))
 
         c_rows = c.rearrange("(p t) j -> p t j", t=PACK)
         c_raw = []
 
-        def load_c(tile, at):
+        def load_c(tile, first_word):
             q = len(c_raw)
-            part = tile[:, at : at + PACK * CHUNK].rearrange("p (t j) -> p t j", t=PACK)
+            part = tile[:, first_word : first_word + PACK * CHUNK].rearrange("p (t j) -> p t j", t=PACK)
             nc.sync.dma_start(out=part, in_=c_rows[:, :, q * CHUNK : (q + 1) * CHUNK])
             c_raw.append(part)
 
         load_c(early, PACK * M)
-        w4 = late.tile([P, 3 * M], U8, name="w4", align_bytes=64, offset=4 * T)
+
+        w4 = placed.tile([P, 3 * M], U8, name="w4", align_bytes=64, offset=W4_AT)
         w4_codes = w4[:, 0 : 2 * M]
         w4_plane = w4[:, 2 * M : 3 * M]
-        nc.gpsimd.memset(w4[:].bitcast(I32), 0)
+        nc.gpsimd.memset(w4_plane.bitcast(I32), 0)
         nc.sync.dma_start(out=w4_codes.bitcast(I32), in_=w4_words[0].bitcast(I32))
-        load_scale_rows((nc.sync,), w4_plane, w4_scales[0])
-        bias = late.tile([P, HALVES], F32, name="bias", offset=4 * T + 3 * M)
+        load_scale_rows(nc, w4_plane, w4_scales[0])
+
+        bias = placed.tile([P, HALVES], F32, name="bias", offset=BIAS_AT)
         with nc.allow_non_contiguous_dma(reason="one bias value for each partition"):
             nc.gpsimd.dma_start(out=bias[:], in_=b.rearrange("(h p) -> p h", p=P))
 
@@ -104,8 +118,8 @@ def tile_list_tabts_bias_kernel(tc, tab_words, tab_scales, w4_words, w4_scales, 
                 nc.tensor.transpose(spread[:, i, :], ts_rows[:, col : col + 1].to_broadcast([P, P]), ident[:])
             nc.scalar.copy(out=ts_groups[:, g], in_=spread[:].rearrange("m i p -> m p i"))
 
-        rest = late.tile([P, rest_words], F32, name="rest", offset=rest_at)
-        for q in range(1, chunks):
+        rest = placed.tile([P, REST_WORDS], F32, name="rest", offset=REST_AT)
+        for q in range(1, CHUNKS):
             load_c(rest, PACK * CHUNK * (q - 1))
 
         picked_scales = keep.tile([P, S], U8, name="picked_scales", align_bytes=64)
@@ -114,41 +128,46 @@ def tile_list_tabts_bias_kernel(tc, tab_words, tab_scales, w4_words, w4_scales, 
         nc.vector.tensor_copy(picked_words[:].bitcast(U32), table_words[:].bitcast(U32).indirect(offsets[:]))
         picked_ts = []
 
-        def pick_ts(j0, width, at):
-            picked = late.tile([P, width], F32, name=f"picked_ts{j0}", offset=at)
+        def pick_ts(first_chunk, chunks, at):
+            j0, width = first_chunk * CHUNK, chunks * CHUNK
+            picked = placed.tile([P, width], F32, name=f"picked_ts{first_chunk}", offset=at)
             nc.vector.tensor_copy(picked[:], ts_all[:].indirect(offsets[:, j0 // 16 : (j0 + width) // 16]))
             for k0 in range(0, width, CHUNK):
                 picked_ts.append(picked[:, k0 : k0 + CHUNK])
 
-        pick_ts(0, BANK, 0)
+        pick_ts(0, 2, WORDS_AT)
 
         u_grouped = keep.tile([P, M, PACK], BF16, name="u_grouped", align_bytes=64)
-        interleave(nc.scalar.copy, u_grouped[:], u_raw)
+        interleave(nc, u_grouped[:], u_raw)
         u_codes = keep.tile([P, M], U32, name="u_codes", align_bytes=64)
         u_plane = keep.tile([P, M], U8, name="u_plane", align_bytes=64)
         nc.vector.quantize_mx(out=u_codes[:].bitcast(FP8X4), scales=u_plane[:], in_=u_grouped[:].rearrange("p n t -> p (n t)"))
 
         c_codes = []
         c_planes = []
-        for q in range(chunks):
-            grouped = late.tile([P, CHUNK, PACK], BF16, name=f"c_grouped{q}", align_bytes=64, offset=grouped_at + 2 * PACK * CHUNK * q)
-            interleave(nc.scalar.copy, grouped[:], c_raw[q])
+        for q in range(CHUNKS):
+            grouped = placed.tile([P, CHUNK, PACK], BF16, name=f"c_grouped{q}", align_bytes=64, offset=GROUPED_AT + GROUPED_BYTES * q)
+            if q < LAST:
+                interleave(nc, grouped[:], c_raw[q])
+            else:
+                cut = CHUNK - SHARE
+                interleave(nc, grouped[:, 0:cut, :], c_raw[q][:, :, 0:cut])
+                nc.gpsimd.tensor_scalar(grouped[:, cut:CHUNK, :], c_raw[q][:, :, cut:CHUNK].rearrange("p t j -> p j t"), 1.0, 0.0, MULT, ADD)
             codes = keep.tile([P, CHUNK], U32, name=f"c_codes{q}", align_bytes=64)
             plane = keep.tile([P, CHUNK], U8, name=f"c_plane{q}", align_bytes=64)
             nc.vector.quantize_mx(out=codes[:].bitcast(FP8X4), scales=plane[:], in_=grouped[:].rearrange("p j t -> p (j t)"))
             c_codes.append(codes)
             c_planes.append(plane)
 
-        pick_ts(2 * CHUNK, CHUNK, grouped_at)
-        pick_ts(3 * CHUNK, CHUNK, grouped_at + 2 * PACK * CHUNK)
+        pick_ts(2, 1, GROUPED_AT)
+        pick_ts(3, 1, GROUPED_AT + GROUPED_BYTES)
 
-        scaled_at = (4 * BANK, 8 * BANK, grouped_at + 2 * PACK * CHUNK * 3, 12 * BANK)
-        results = keep.tile([P, chunks, CHUNK], F32, name="results")
+        scaled_at = (WORDS_AT + SCALED_BYTES, WORDS_AT + 2 * SCALED_BYTES, GROUPED_AT + GROUPED_BYTES * LAST, WORDS_AT + 3 * SCALED_BYTES)
         sums = []
 
         def table_passes(q):
             for h in range(HALVES):
-                acc = psum.tile([P, CHUNK], F32, name=f"acc{q}{h}", tag=f"bank{(4, 6, 0, 4)[q] + h}")
+                acc = psum.tile([P, CHUNK], F32, name=f"acc{q}{h}", tag=f"bank{SUM_BANKS[q] + h}")
                 for k0 in range(0, CHUNK, P):
                     cols = slice(q * CHUNK + k0, q * CHUNK + k0 + P)
                     nc.tensor.matmul_mx(
@@ -173,26 +192,24 @@ def tile_list_tabts_bias_kernel(tc, tab_words, tab_scales, w4_words, w4_scales, 
                     start=False,
                     stop=True,
                 )
-            scaled = late.tile([P, HALVES, CHUNK], F32, name=f"scaled{q}", align_bytes=64, offset=scaled_at[q])
+            scaled = placed.tile([P, HALVES, CHUNK], F32, name=f"scaled{q}", align_bytes=64, offset=scaled_at[q])
             for h in range(HALVES):
-                result = results[:, q, :] if h == 0 else rest[:, rest_words - (q + 1) * CHUNK : rest_words - q * CHUNK]
-                last = q == chunks - 1 and h == HALVES - 1
-                width = CHUNK // 2 if last else CHUNK
-                for k0 in range(0, CHUNK, width):
-                    here = slice(k0, k0 + width)
-                    nc.vector.tensor_tensor(scaled[:, h, here], sums[q * HALVES + h][:, here], picked_ts[q][:, here], MULT)
-                    if h == 0 and q < chunks - 1:
-                        nc.gpsimd.tensor_scalar(result[:, here], scaled[:, h, here], 1.0, bias[:, h : h + 1], MULT, ADD)
-                    else:
-                        nc.scalar.activation(result[:, here], scaled[:, h, here], IDENT, bias=bias[:, h : h + 1])
-                    queue = nc.scalar if last and k0 > 0 else nc.sync
-                    queue.dma_start(out=out[h * P : (h + 1) * P, q * CHUNK + k0 : q * CHUNK + k0 + width], in_=result[:, here])
+                n = q * HALVES + h
+                if 1 <= n <= 3:
+                    result = rest[:, REST_WORDS - n * CHUNK : REST_WORDS - (n - 1) * CHUNK]
+                else:
+                    result = keep.tile([P, CHUNK], F32, name=f"result{n}")[:]
+                nc.vector.tensor_tensor(scaled[:, h, :], sums[n][:], picked_ts[q], MULT)
+                if h == 0 and q < LAST:
+                    nc.gpsimd.tensor_scalar(result, scaled[:, h, :], 1.0, bias[:, h : h + 1], MULT, ADD)
+                else:
+                    nc.scalar.activation(result, scaled[:, h, :], IDENT, bias=bias[:, h : h + 1])
+                queue = nc.scalar if n == CHUNKS * HALVES - 1 else nc.sync
+                queue.dma_start(out=out[h * P : (h + 1) * P, q * CHUNK : (q + 1) * CHUNK], in_=result)
 
-        table_passes(0)
-        table_passes(1)
-        table_passes(2)
+        for q in range(LAST):
+            table_passes(q)
         finish(0)
-        table_passes(3)
-        finish(1)
-        finish(2)
-        finish(3)
+        table_passes(LAST)
+        for q in range(1, CHUNKS):
+            finish(q)

@@ -42,9 +42,9 @@ GATE_WORDS = (EARLY_AT + 32 - GATE_AT) // 4
 SUM_BANKS = (4, 6, 0, 4)
 
 
-def load_scale_rows(nc, plane, rows):
+def load_scale_rows(queues, plane, rows):
     for q in range(4):
-        nc.sync.dma_start(out=plane[32 * q : 32 * q + 4, :].bitcast(I32), in_=rows[4 * q : 4 * q + 4, :].bitcast(I32))
+        queues[q % len(queues)].dma_start(out=plane[32 * q : 32 * q + 4, :].bitcast(I32), in_=rows[4 * q : 4 * q + 4, :].bitcast(I32))
 
 
 def interleave(nc, grouped, raw):
@@ -68,8 +68,8 @@ def tile_list_tabts_bias_kernel(tc, tab_words, tab_scales, w4_words, w4_scales, 
         nc.sync.dma_start(out=ts_rows[:], in_=ts[0].rearrange("(p i) -> p i", i=TS_ROW))
 
         table_scales = keep.tile([P, T], U8, name="table_scales", align_bytes=64)
-        nc.gpsimd.memset(table_scales[:].bitcast(I32), 0)
-        load_scale_rows(nc, table_scales, tab_scales[0])
+        nc.vector.memset(table_scales[:].bitcast(I32), 0)
+        load_scale_rows((nc.sync, nc.scalar), table_scales, tab_scales[0])
 
         gate = placed.tile([P, GATE_WORDS], F32, name="gate", offset=GATE_AT)
         zeros = gate[:, 0:P]
@@ -103,7 +103,7 @@ def tile_list_tabts_bias_kernel(tc, tab_words, tab_scales, w4_words, w4_scales, 
         w4_plane = w4[:, 2 * M : 3 * M]
         nc.gpsimd.memset(w4_plane.bitcast(I32), 0)
         nc.sync.dma_start(out=w4_codes.bitcast(I32), in_=w4_words[0].bitcast(I32))
-        load_scale_rows(nc, w4_plane, w4_scales[0])
+        load_scale_rows((nc.sync,), w4_plane, w4_scales[0])
 
         bias = placed.tile([P, HALVES], F32, name="bias", offset=BIAS_AT)
         with nc.allow_non_contiguous_dma(reason="one bias value for each partition"):

@@ -33,13 +33,14 @@ EARLY_AT = BIAS_AT + 32
 EARLY_WORDS = PACK * (M + CHUNK)
 REST_AT = EARLY_AT + 4 * EARLY_WORDS
 REST_WORDS = PACK * (S - CHUNK)
-GROUPED_AT = REST_AT + 4 * REST_WORDS + 32
+GROUPED_AT = REST_AT + 4 * (REST_WORDS + 64) + 32
 GROUPED_BYTES = 2 * PACK * CHUNK
 SCALED_BYTES = 4 * HALVES * CHUNK
+CODES_AT = GROUPED_AT + CHUNKS * GROUPED_BYTES
 GATE_AT = W4_AT - 64
 GATE_WORDS = (EARLY_AT + 32 - GATE_AT) // 4
 
-SUM_BANKS = (4, 6, 0, 4)
+SUM_BANKS = (4, 6, 0, 6)
 
 
 def load_scale_rows(queues, plane, rows):
@@ -118,7 +119,7 @@ def tile_list_tabts_bias_kernel(tc, tab_words, tab_scales, w4_words, w4_scales, 
                 nc.tensor.transpose(spread[:, i, :], ts_rows[:, col : col + 1].to_broadcast([P, P]), ident[:])
             nc.scalar.copy(out=ts_groups[:, g], in_=spread[:].rearrange("m i p -> m p i"))
 
-        rest = placed.tile([P, REST_WORDS], F32, name="rest", offset=REST_AT)
+        rest = placed.tile([P, REST_WORDS + 64], F32, name="rest", offset=REST_AT)
         for q in range(1, CHUNKS):
             load_c(rest, PACK * CHUNK * (q - 1))
 
@@ -128,14 +129,13 @@ def tile_list_tabts_bias_kernel(tc, tab_words, tab_scales, w4_words, w4_scales, 
         nc.vector.tensor_copy(picked_words[:].bitcast(U32), table_words[:].bitcast(U32).indirect(offsets[:]))
         picked_ts = []
 
-        def pick_ts(first_chunk, chunks, at):
+        def pick_ts(first_chunk, chunks, picked):
             j0, width = first_chunk * CHUNK, chunks * CHUNK
-            picked = placed.tile([P, width], F32, name=f"picked_ts{first_chunk}", offset=at)
-            nc.vector.tensor_copy(picked[:], ts_all[:].indirect(offsets[:, j0 // 16 : (j0 + width) // 16]))
+            nc.vector.tensor_copy(picked, ts_all[:].indirect(offsets[:, j0 // 16 : (j0 + width) // 16]))
             for k0 in range(0, width, CHUNK):
                 picked_ts.append(picked[:, k0 : k0 + CHUNK])
 
-        pick_ts(0, 2, WORDS_AT)
+        pick_ts(0, 2, keep.tile([P, 2 * CHUNK], F32, name="picked_ts")[:])
 
         u_grouped = keep.tile([P, M, PACK], BF16, name="u_grouped", align_bytes=64)
         interleave(nc, u_grouped[:], u_raw)
@@ -147,22 +147,17 @@ def tile_list_tabts_bias_kernel(tc, tab_words, tab_scales, w4_words, w4_scales, 
         c_planes = []
         for q in range(CHUNKS):
             grouped = placed.tile([P, CHUNK, PACK], BF16, name=f"c_grouped{q}", align_bytes=64, offset=GROUPED_AT + GROUPED_BYTES * q)
-            if q < LAST:
-                interleave(nc, grouped[:], c_raw[q])
-            else:
-                cut = CHUNK - SHARE
-                interleave(nc, grouped[:, 0:cut, :], c_raw[q][:, :, 0:cut])
-                nc.gpsimd.tensor_scalar(grouped[:, cut:CHUNK, :], c_raw[q][:, :, cut:CHUNK].rearrange("p t j -> p j t"), 1.0, 0.0, MULT, ADD)
-            codes = keep.tile([P, CHUNK], U32, name=f"c_codes{q}", align_bytes=64)
+            interleave(nc, grouped[:], c_raw[q])
+            codes = placed.tile([P, CHUNK], U32, name=f"c_codes{q}", align_bytes=64, offset=CODES_AT + 4 * CHUNK * q)
             plane = keep.tile([P, CHUNK], U8, name=f"c_plane{q}", align_bytes=64)
             nc.vector.quantize_mx(out=codes[:].bitcast(FP8X4), scales=plane[:], in_=grouped[:].rearrange("p j t -> p (j t)"))
             c_codes.append(codes)
             c_planes.append(plane)
 
-        pick_ts(2, 1, GROUPED_AT)
-        pick_ts(3, 1, GROUPED_AT + GROUPED_BYTES)
+        pick_ts(2, 1, early[:, PACK * M : PACK * M + CHUNK])
 
         scaled_at = (WORDS_AT + SCALED_BYTES, WORDS_AT + 2 * SCALED_BYTES, GROUPED_AT + GROUPED_BYTES * LAST, WORDS_AT + 3 * SCALED_BYTES)
+        behind_last = REST_WORDS - 4 * CHUNK
         sums = []
 
         def table_passes(q):
@@ -192,11 +187,18 @@ def tile_list_tabts_bias_kernel(tc, tab_words, tab_scales, w4_words, w4_scales, 
                     start=False,
                     stop=True,
                 )
-            scaled = placed.tile([P, HALVES, CHUNK], F32, name=f"scaled{q}", align_bytes=64, offset=scaled_at[q])
+            if q == 2:
+                scaled = rest[:, behind_last : behind_last + 2 * CHUNK].rearrange("p (h j) -> p h j", h=HALVES)
+            elif q < 2:
+                scaled = rest[:, q * PACK * CHUNK : (q * PACK + 2) * CHUNK].rearrange("p (h j) -> p h j", h=HALVES)
+            else:
+                scaled = keep.tile([P, HALVES, CHUNK], F32, name="scaled_last")
             for h in range(HALVES):
                 n = q * HALVES + h
-                if 1 <= n <= 3:
-                    result = rest[:, REST_WORDS - n * CHUNK : REST_WORDS - (n - 1) * CHUNK]
+                if n in (1, 3):
+                    result = rest[:, behind_last + (2 + n // 2) * CHUNK : behind_last + (3 + n // 2) * CHUNK]
+                elif n == 2:
+                    result = placed.tile([P, CHUNK], F32, name="result2", offset=GROUPED_AT + LAST * GROUPED_BYTES)[:]
                 else:
                     result = keep.tile([P, CHUNK], F32, name=f"result{n}")[:]
                 nc.vector.tensor_tensor(scaled[:, h, :], sums[n][:], picked_ts[q], MULT)
@@ -207,9 +209,12 @@ def tile_list_tabts_bias_kernel(tc, tab_words, tab_scales, w4_words, w4_scales, 
                 queue = nc.scalar if n == CHUNKS * HALVES - 1 else nc.sync
                 queue.dma_start(out=out[h * P : (h + 1) * P, q * CHUNK : (q + 1) * CHUNK], in_=result)
 
-        for q in range(LAST):
-            table_passes(q)
+        table_passes(0)
         finish(0)
+        pick_ts(3, 1, rest[:, 2 * CHUNK : 3 * CHUNK])
+        table_passes(1)
+        table_passes(2)
+        finish(1)
         table_passes(LAST)
-        for q in range(1, CHUNKS):
-            finish(q)
+        finish(2)
+        finish(LAST)

@@ -28,12 +28,12 @@ SHARE = 64
 
 WORDS_AT = 0
 W4_AT = WORDS_AT + 4 * T
-BIAS_AT = W4_AT + 3 * M
-EARLY_AT = BIAS_AT + 32
+BIAS_AT = W4_AT + M
+EARLY_AT = BIAS_AT + 4 * P
 EARLY_WORDS = PACK * (M + CHUNK)
 REST_AT = EARLY_AT + 4 * EARLY_WORDS
 REST_WORDS = PACK * (S - CHUNK)
-GROUPED_AT = REST_AT + 4 * (REST_WORDS + 64) + 32
+GROUPED_AT = REST_AT + 4 * (REST_WORDS + 64)
 GROUPED_BYTES = 2 * PACK * CHUNK
 SCALED_BYTES = 4 * HALVES * CHUNK
 CODES_AT = GROUPED_AT + CHUNKS * GROUPED_BYTES
@@ -68,6 +68,9 @@ def tile_list_tabts_bias_kernel(tc, tab_words, tab_scales, w4_words, w4_scales, 
         ts_rows = placed.tile([P, TS_ROW], F32, name="ts_rows", offset=REST_AT)
         nc.sync.dma_start(out=ts_rows[:], in_=ts[0].rearrange("(p i) -> p i", i=TS_ROW))
 
+        w4_codes = keep.tile([P, 2 * M], U8, name="w4_codes", align_bytes=64)[:]
+        nc.sync.dma_start(out=w4_codes.bitcast(I32), in_=w4_words[0].bitcast(I32))
+
         table_scales = keep.tile([P, T], U8, name="table_scales", align_bytes=64)
         nc.vector.memset(table_scales[:].bitcast(I32), 0)
         load_scale_rows((nc.sync, nc.scalar), table_scales, tab_scales[0])
@@ -99,16 +102,13 @@ def tile_list_tabts_bias_kernel(tc, tab_words, tab_scales, w4_words, w4_scales, 
 
         load_c(early, PACK * M)
 
-        w4 = placed.tile([P, 3 * M], U8, name="w4", align_bytes=64, offset=W4_AT)
-        w4_codes = w4[:, 0 : 2 * M]
-        w4_plane = w4[:, 2 * M : 3 * M]
+        w4_plane = placed.tile([P, M], U8, name="w4_plane", align_bytes=64, offset=W4_AT)[:]
         nc.gpsimd.memset(w4_plane.bitcast(I32), 0)
-        nc.sync.dma_start(out=w4_codes.bitcast(I32), in_=w4_words[0].bitcast(I32))
         load_scale_rows((nc.sync,), w4_plane, w4_scales[0])
 
-        bias = placed.tile([P, HALVES], F32, name="bias", offset=BIAS_AT)
-        with nc.allow_non_contiguous_dma(reason="one bias value for each partition"):
-            nc.gpsimd.dma_start(out=bias[:], in_=b.rearrange("(h p) -> p h", p=P))
+        bias_rows = placed.tile([P, P], F32, name="bias_rows", offset=BIAS_AT)
+        nc.gpsimd.memset(bias_rows[:], 0.0)
+        nc.gpsimd.dma_start(out=bias_rows[0:HALVES, :], in_=b.rearrange("(h p) -> h p", p=P))
 
         ts_all = keep.tile([P, T], F32, name="ts_all")
         ts_groups = ts_all[:].rearrange("m (p g i) -> m g p i", g=4, i=4)
@@ -118,6 +118,9 @@ def tile_list_tabts_bias_kernel(tc, tab_words, tab_scales, w4_words, w4_scales, 
                 col = 4 * g + i
                 nc.tensor.transpose(spread[:, i, :], ts_rows[:, col : col + 1].to_broadcast([P, P]), ident[:])
             nc.scalar.copy(out=ts_groups[:, g], in_=spread[:].rearrange("m i p -> m p i"))
+
+        bias_turned = psum.tile([P, P], F32, name="bias_turned", tag="bank3")
+        nc.tensor.transpose(bias_turned[:], bias_rows[:], ident[:])
 
         rest = placed.tile([P, REST_WORDS + 64], F32, name="rest", offset=REST_AT)
         for q in range(1, CHUNKS):
@@ -145,14 +148,26 @@ def tile_list_tabts_bias_kernel(tc, tab_words, tab_scales, w4_words, w4_scales, 
 
         c_codes = []
         c_planes = []
+        pair = placed.tile([P, 2 * CHUNK - SHARE, PACK], BF16, name="pair", align_bytes=64, offset=GROUPED_AT + GROUPED_BYTES * 2)
+        cut = CHUNK - SHARE
         for q in range(CHUNKS):
-            grouped = placed.tile([P, CHUNK, PACK], BF16, name=f"c_grouped{q}", align_bytes=64, offset=GROUPED_AT + GROUPED_BYTES * q)
-            interleave(nc, grouped[:], c_raw[q])
+            if q < 2:
+                grouped = keep.tile([P, CHUNK, PACK], BF16, name=f"c_grouped{q}", align_bytes=64)[:]
+            else:
+                grouped = pair[:, cut * (LAST - q) : cut * (LAST - q) + CHUNK, :]
+            if q < LAST:
+                interleave(nc, grouped, c_raw[q])
+            else:
+                interleave(nc, grouped[:, 0:cut, :], c_raw[q][:, :, 0:cut])
+                nc.gpsimd.tensor_scalar(grouped[:, cut:CHUNK, :], c_raw[q][:, :, cut:CHUNK].rearrange("p t j -> p j t"), 1.0, 0.0, MULT, ADD)
             codes = placed.tile([P, CHUNK], U32, name=f"c_codes{q}", align_bytes=64, offset=CODES_AT + 4 * CHUNK * q)
             plane = keep.tile([P, CHUNK], U8, name=f"c_plane{q}", align_bytes=64)
-            nc.vector.quantize_mx(out=codes[:].bitcast(FP8X4), scales=plane[:], in_=grouped[:].rearrange("p j t -> p (j t)"))
+            nc.vector.quantize_mx(out=codes[:].bitcast(FP8X4), scales=plane[:], in_=grouped.rearrange("p j t -> p (j t)"))
             c_codes.append(codes)
             c_planes.append(plane)
+
+        bias = early[:, EARLY_WORDS - 8 : EARLY_WORDS - 8 + HALVES]
+        nc.scalar.copy(out=bias, in_=bias_turned[:, 0:HALVES])
 
         pick_ts(2, 1, early[:, PACK * M : PACK * M + CHUNK])
 
@@ -198,7 +213,7 @@ def tile_list_tabts_bias_kernel(tc, tab_words, tab_scales, w4_words, w4_scales, 
                 if n in (1, 3):
                     result = rest[:, behind_last + (2 + n // 2) * CHUNK : behind_last + (3 + n // 2) * CHUNK]
                 elif n == 2:
-                    result = placed.tile([P, CHUNK], F32, name="result2", offset=GROUPED_AT + LAST * GROUPED_BYTES)[:]
+                    result = placed.tile([P, CHUNK], F32, name="result2", offset=GROUPED_AT + 2 * GROUPED_BYTES)[:]
                 else:
                     result = keep.tile([P, CHUNK], F32, name=f"result{n}")[:]
                 nc.vector.tensor_tensor(scaled[:, h, :], sums[n][:], picked_ts[q], MULT)

@@ -172,7 +172,7 @@ def tile_list_tabts_bias_kernel(tc, tab_words, tab_scales, w4_words, w4_scales, 
         pick_ts(2, 1, early[:, PACK * M : PACK * M + CHUNK])
 
         scaled_at = (WORDS_AT + SCALED_BYTES, WORDS_AT + 2 * SCALED_BYTES, GROUPED_AT + GROUPED_BYTES * LAST, WORDS_AT + 3 * SCALED_BYTES)
-        behind_last = REST_WORDS - 4 * CHUNK
+        behind_last = REST_WORDS + 64 - 5 * CHUNK
         sums = []
 
         def table_passes(q):
@@ -210,14 +210,12 @@ def tile_list_tabts_bias_kernel(tc, tab_words, tab_scales, w4_words, w4_scales, 
                 scaled = keep.tile([P, HALVES, CHUNK], F32, name="scaled_last")
             for h in range(HALVES):
                 n = q * HALVES + h
-                if n in (1, 3):
-                    result = rest[:, behind_last + (2 + n // 2) * CHUNK : behind_last + (3 + n // 2) * CHUNK]
-                elif n == 2:
-                    result = placed.tile([P, CHUNK], F32, name="result2", offset=GROUPED_AT + 2 * GROUPED_BYTES)[:]
+                if 1 <= n <= 3:
+                    result = rest[:, behind_last + (1 + n) * CHUNK : behind_last + (2 + n) * CHUNK]
                 else:
                     result = keep.tile([P, CHUNK], F32, name=f"result{n}")[:]
                 nc.vector.tensor_tensor(scaled[:, h, :], sums[n][:], picked_ts[q], MULT)
-                if h == 0 and q < LAST:
+                if h == 0 and q in (0, 2):
                     nc.gpsimd.tensor_scalar(result, scaled[:, h, :], 1.0, bias[:, h : h + 1], MULT, ADD)
                 else:
                     nc.scalar.activation(result, scaled[:, h, :], IDENT, bias=bias[:, h : h + 1])

@@ -214,8 +214,8 @@ def tile_list_tabts_bias_kernel(tc, tab_words, tab_scales, w4_words, w4_scales, 
                     result = rest[:, behind_last + (1 + n) * CHUNK : behind_last + (2 + n) * CHUNK]
                 else:
                     result = keep.tile([P, CHUNK], F32, name=f"result{n}")[:]
-                nc.vector.tensor_tensor(scaled[:, h, :], sums[n][:], picked_ts[q], MULT)
-                if h == 0 and q in (0, 2):
+                nc.vector.tensor_tensor(scaled[:, h, :], picked_ts[q], sums[n][:], MULT)
+                if n == 0:
                     nc.gpsimd.tensor_scalar(result, scaled[:, h, :], 1.0, bias[:, h : h + 1], MULT, ADD)
                 else:
                     nc.scalar.activation(result, scaled[:, h, :], IDENT, bias=bias[:, h : h + 1])

@@ -14,7 +14,6 @@ U8 = mybir.dt.uint8
 FP8X4 = mybir.dt.float8_e4m3fn_x4
 FP4X4 = mybir.dt.float4_e2m1fn_x4
 MULT = mybir.AluOpType.mult
-ADD = mybir.AluOpType.add
 IDENT = mybir.ActivationFunctionType.Identity
 
 P = 128
@@ -22,30 +21,28 @@ PACK = 4
 HALVES = M // P
 CHUNK = 256
 CHUNKS = S // CHUNK
-LAST = CHUNKS - 1
-TS_ROW = T // P
-SHARE = 64
+BANK = 512
+RAW = 4 * PACK * CHUNK
 
-WORDS_AT = 0
+COLUMNS_AT = 0
+C0_AT = COLUMNS_AT + RAW // 2
+C2_AT = C0_AT + RAW + 64
+C3_AT = C2_AT + RAW
+RESULTS_AT = C3_AT + RAW
+GATE_AT = RESULTS_AT + RAW
+C1_AT = GATE_AT + 4 * P
+WORDS_AT = C1_AT + RAW
 W4_AT = WORDS_AT + 4 * T
-BIAS_AT = W4_AT + M
-EARLY_AT = BIAS_AT + 4 * P
-EARLY_WORDS = PACK * (M + CHUNK)
-REST_AT = EARLY_AT + 4 * EARLY_WORDS
-REST_WORDS = PACK * (S - CHUNK)
-GROUPED_AT = REST_AT + 4 * (REST_WORDS + 64)
-GROUPED_BYTES = 2 * PACK * CHUNK
-SCALED_BYTES = 4 * HALVES * CHUNK
-CODES_AT = GROUPED_AT + CHUNKS * GROUPED_BYTES
-GATE_AT = W4_AT - 64
-GATE_WORDS = (EARLY_AT + 32 - GATE_AT) // 4
-
-SUM_BANKS = (4, 6, 0, 6)
+W4_PLANE_AT = W4_AT + 2 * M
+GATE_END = W4_PLANE_AT + M
+PICKED_AT = GATE_END
+SUM_BANKS = (2, 4, 6, 0)
+CLEAR_SPLIT = 1256
 
 
-def load_scale_rows(queues, plane, rows):
+def load_scale_rows(nc, plane, rows):
     for q in range(4):
-        queues[q % len(queues)].dma_start(out=plane[32 * q : 32 * q + 4, :].bitcast(I32), in_=rows[4 * q : 4 * q + 4, :].bitcast(I32))
+        nc.sync.dma_start(out=plane[32 * q : 32 * q + 4, :].bitcast(I32), in_=rows[4 * q : 4 * q + 4, :].bitcast(I32))
 
 
 def interleave(nc, grouped, raw):
@@ -65,17 +62,28 @@ def tile_list_tabts_bias_kernel(tc, tab_words, tab_scales, w4_words, w4_scales, 
         offsets = keep.tile([P, S // 16], U16, name="offsets")
         nc.sync.dma_start(offsets[:], offs)
 
-        ts_rows = placed.tile([P, TS_ROW], F32, name="ts_rows", offset=REST_AT)
-        nc.sync.dma_start(out=ts_rows[:], in_=ts[0].rearrange("(p i) -> p i", i=TS_ROW))
+        ts_window = keep.tile([P, T], F32, name="ts_window")
+        nc.sync.dma_start(out=ts_window[P - 1 : P, :], in_=ts[0:1, :])
 
-        w4_codes = keep.tile([P, 2 * M], U8, name="w4_codes", align_bytes=64)[:]
-        nc.sync.dma_start(out=w4_codes.bitcast(I32), in_=w4_words[0].bitcast(I32))
+        u_raw = keep.tile([P, PACK, M], F32, name="u_raw")[:]
+        nc.sync.dma_start(out=u_raw, in_=u.rearrange("(p t) n -> p t n", t=PACK))
+
+        c_rows = c.rearrange("(p t) j -> p t j", t=PACK)
+
+        def load_c(q, at):
+            rim = {0: (RAW + 96) // 4, 3: RAW // 4}.get(q, 0)
+            tile = placed.tile([P, PACK * CHUNK + rim], F32, name=f"c_raw{q}", offset=at)
+            raw = tile[:, 0 : PACK * CHUNK].rearrange("p (t j) -> p t j", t=PACK)
+            nc.sync.dma_start(out=raw, in_=c_rows[:, :, q * CHUNK : (q + 1) * CHUNK])
+            return raw
+
+        c_raw = [load_c(0, C0_AT)]
 
         table_scales = keep.tile([P, T], U8, name="table_scales", align_bytes=64)
         nc.vector.memset(table_scales[:].bitcast(I32), 0)
-        load_scale_rows((nc.sync, nc.scalar), table_scales, tab_scales[0])
+        load_scale_rows(nc, table_scales, tab_scales[0])
 
-        gate = placed.tile([P, GATE_WORDS], F32, name="gate", offset=GATE_AT)
+        gate = placed.tile([P, (GATE_END - GATE_AT) // 4], F32, name="gate", offset=GATE_AT)
         zeros = gate[:, 0:P]
         nc.vector.memset(zeros, 0.0)
         ident = keep.tile([P, P], F32, name="ident")
@@ -83,151 +91,162 @@ def tile_list_tabts_bias_kernel(tc, tab_words, tab_scales, w4_words, w4_scales, 
             out=ident[:], in_=zeros, pattern=[[-1, P]], compare_op=mybir.AluOpType.not_equal,
             fill=1.0, base=0, channel_multiplier=1,
         )
+        nc.vector.memset(ts_window[0 : P - 1, 0 : CLEAR_SPLIT - 7], 0.0)
+        nc.vector.memset(ts_window[0 : P - 1, CLEAR_SPLIT - 7 : CLEAR_SPLIT], 0.0)
+        nc.gpsimd.memset(ts_window[0 : P - 1, CLEAR_SPLIT:T], 0.0)
+
 
         table_words = placed.tile([P, T], I32, name="table_words", align_bytes=64, offset=WORDS_AT)
         nc.sync.dma_start(out=table_words[:], in_=tab_words[0].rearrange("p t i -> p (t i)").bitcast(I32))
 
-        early = placed.tile([P, EARLY_WORDS], F32, name="early", offset=EARLY_AT)
-        u_raw = early[:, 0 : PACK * M].rearrange("p (t n) -> p t n", t=PACK)
-        nc.sync.dma_start(out=u_raw, in_=u.rearrange("(p t) n -> p t n", t=PACK))
+        c_raw.append(load_c(1, C1_AT))
 
-        c_rows = c.rearrange("(p t) j -> p t j", t=PACK)
-        c_raw = []
-
-        def load_c(tile, first_word):
-            q = len(c_raw)
-            part = tile[:, first_word : first_word + PACK * CHUNK].rearrange("p (t j) -> p t j", t=PACK)
-            nc.sync.dma_start(out=part, in_=c_rows[:, :, q * CHUNK : (q + 1) * CHUNK])
-            c_raw.append(part)
-
-        load_c(early, PACK * M)
-
-        w4_plane = placed.tile([P, M], U8, name="w4_plane", align_bytes=64, offset=W4_AT)[:]
+        w4_codes = placed.tile([P, 2 * M], U8, name="w4_codes", align_bytes=64, offset=W4_AT)[:]
+        nc.sync.dma_start(out=w4_codes.bitcast(I32), in_=w4_words[0].bitcast(I32))
+        w4_plane = placed.tile([P, M], U8, name="w4_plane", align_bytes=64, offset=W4_PLANE_AT)[:]
         nc.gpsimd.memset(w4_plane.bitcast(I32), 0)
-        load_scale_rows((nc.sync,), w4_plane, w4_scales[0])
+        load_scale_rows(nc, w4_plane, w4_scales[0])
 
-        bias_rows = placed.tile([P, P], F32, name="bias_rows", offset=BIAS_AT)
-        nc.gpsimd.memset(bias_rows[:], 0.0)
-        nc.gpsimd.dma_start(out=bias_rows[0:HALVES, :], in_=b.rearrange("(h p) -> h p", p=P))
+        bias_rows = keep.tile([P, P], F32, name="bias_rows")
+        nc.gpsimd.memset(bias_rows[0 : P - HALVES, :], 0.0)
+        nc.sync.dma_start(out=bias_rows[P - HALVES : P, :], in_=b.rearrange("(h p) -> h p", p=P))
 
-        ts_all = keep.tile([P, T], F32, name="ts_all")
-        ts_groups = ts_all[:].rearrange("m (p g i) -> m g p i", g=4, i=4)
-        for g in range(4):
-            spread = psum.tile([P, 4, P], F32, name=f"spread{g}", tag=f"bank{g}")
-            for i in range(4):
-                col = 4 * g + i
-                nc.tensor.transpose(spread[:, i, :], ts_rows[:, col : col + 1].to_broadcast([P, P]), ident[:])
-            nc.scalar.copy(out=ts_groups[:, g], in_=spread[:].rearrange("m i p -> m p i"))
-
-        bias_turned = psum.tile([P, P], F32, name="bias_turned", tag="bank3")
-        nc.tensor.transpose(bias_turned[:], bias_rows[:], ident[:])
-
-        rest = placed.tile([P, REST_WORDS + 64], F32, name="rest", offset=REST_AT)
-        for q in range(1, CHUNKS):
-            load_c(rest, PACK * CHUNK * (q - 1))
-
+        picked_ts = []
+        for g in range(2):
+            picked = keep.tile([P, BANK], F32, name=f"picked_ts{g}")
+            nc.vector.tensor_copy(picked[:], ts_window[:].indirect(offsets[:, g * BANK // 16 : (g + 1) * BANK // 16]))
+            picked_ts.append(picked)
         picked_scales = keep.tile([P, S], U8, name="picked_scales", align_bytes=64)
         nc.vector.tensor_copy(picked_scales[:], table_scales[:].indirect(offsets[:]))
-        picked_words = keep.tile([P, S], I32, name="picked_words", align_bytes=64)
-        nc.vector.tensor_copy(picked_words[:].bitcast(U32), table_words[:].bitcast(U32).indirect(offsets[:]))
-        picked_ts = []
 
-        def pick_ts(first_chunk, chunks, picked):
-            j0, width = first_chunk * CHUNK, chunks * CHUNK
-            nc.vector.tensor_copy(picked, ts_all[:].indirect(offsets[:, j0 // 16 : (j0 + width) // 16]))
-            for k0 in range(0, width, CHUNK):
-                picked_ts.append(picked[:, k0 : k0 + CHUNK])
+        first = keep.tile([P, M + CHUNK, PACK], BF16, name="first", align_bytes=64)
+        interleave(nc, first[:, 0:M, :], u_raw)
+        interleave(nc, first[:, M : M + CHUNK, :], c_raw[0])
+        first_codes = keep.tile([P, M + CHUNK], U32, name="first_codes", align_bytes=64)
+        first_plane = keep.tile([P, M + CHUNK], U8, name="first_plane", align_bytes=64)
+        nc.vector.quantize_mx(out=first_codes[:].bitcast(FP8X4), scales=first_plane[:], in_=first[:].rearrange("p n t -> p (n t)"))
+        c_codes = [first_codes[:, M : M + CHUNK]]
+        c_planes = [first_plane[:, M : M + CHUNK]]
 
-        pick_ts(0, 2, keep.tile([P, 2 * CHUNK], F32, name="picked_ts")[:])
+        def round_c(q):
+            grouped = placed.tile([P, CHUNK, PACK], BF16, name=f"c_grouped{q}", align_bytes=64, offset=COLUMNS_AT + (q - 1) * RAW // 2)
+            interleave(nc, grouped[:], c_raw[q])
+            return grouped
 
-        u_grouped = keep.tile([P, M, PACK], BF16, name="u_grouped", align_bytes=64)
-        interleave(nc, u_grouped[:], u_raw)
-        u_codes = keep.tile([P, M], U32, name="u_codes", align_bytes=64)
-        u_plane = keep.tile([P, M], U8, name="u_plane", align_bytes=64)
-        nc.vector.quantize_mx(out=u_codes[:].bitcast(FP8X4), scales=u_plane[:], in_=u_grouped[:].rearrange("p n t -> p (n t)"))
-
-        c_codes = []
-        c_planes = []
-        pair = placed.tile([P, 2 * CHUNK - SHARE, PACK], BF16, name="pair", align_bytes=64, offset=GROUPED_AT + GROUPED_BYTES * 2)
-        cut = CHUNK - SHARE
-        for q in range(CHUNKS):
-            if q < 2:
-                grouped = keep.tile([P, CHUNK, PACK], BF16, name=f"c_grouped{q}", align_bytes=64)[:]
-            else:
-                grouped = pair[:, cut * (LAST - q) : cut * (LAST - q) + CHUNK, :]
-            if q < LAST:
-                interleave(nc, grouped, c_raw[q])
-            else:
-                interleave(nc, grouped[:, 0:cut, :], c_raw[q][:, :, 0:cut])
-                nc.gpsimd.tensor_scalar(grouped[:, cut:CHUNK, :], c_raw[q][:, :, cut:CHUNK].rearrange("p t j -> p j t"), 1.0, 0.0, MULT, ADD)
-            codes = placed.tile([P, CHUNK], U32, name=f"c_codes{q}", align_bytes=64, offset=CODES_AT + 4 * CHUNK * q)
+        def quantise_c(q, grouped):
+            codes = keep.tile([P, CHUNK], U32, name=f"c_codes{q}", align_bytes=64)
             plane = keep.tile([P, CHUNK], U8, name=f"c_plane{q}", align_bytes=64)
-            nc.vector.quantize_mx(out=codes[:].bitcast(FP8X4), scales=plane[:], in_=grouped.rearrange("p j t -> p (j t)"))
-            c_codes.append(codes)
-            c_planes.append(plane)
+            nc.vector.quantize_mx(out=codes[:].bitcast(FP8X4), scales=plane[:], in_=grouped[:].rearrange("p j t -> p (j t)"))
+            c_codes.append(codes[:])
+            c_planes.append(plane[:])
 
-        bias = early[:, EARLY_WORDS - 8 : EARLY_WORDS - 8 + HALVES]
-        nc.scalar.copy(out=bias, in_=bias_turned[:, 0:HALVES])
+        bias_turned = psum.tile([P, P], F32, name="bias_turned", tag="bank7")
+        nc.tensor.transpose(bias_turned[:], bias_rows[:], ident[:])
+        bias = placed.tile([P, HALVES], F32, name="bias", offset=C2_AT - 32)[:]
 
-        pick_ts(2, 1, early[:, PACK * M : PACK * M + CHUNK])
+        ts_wide = []
+        ts_columns = placed.tile([P, (RAW + 32) // 4], F32, name="ts_columns", offset=COLUMNS_AT)
 
-        scaled_at = (WORDS_AT + SCALED_BYTES, WORDS_AT + 2 * SCALED_BYTES, GROUPED_AT + GROUPED_BYTES * LAST, WORDS_AT + 3 * SCALED_BYTES)
-        behind_last = REST_WORDS + 64 - 5 * CHUNK
-        sums = []
+        def turn_ts(g):
+            turned = psum.tile([P, 4, P], F32, name=f"turned{g}", tag=f"bank{g}")
+            for i in range(4):
+                nc.tensor.transpose(turned[:, i, :], picked_ts[g][:, i * P : (i + 1) * P], ident[:])
+            columns = ts_columns[:, 8 * g : 8 * g + 4]
+            nc.scalar.copy(out=columns, in_=turned[:, :, P - 1])
+            return columns
 
-        def table_passes(q):
+        def spread_ts(g, columns):
+            for q in range(2 * g, 2 * g + 2):
+                spread = psum.tile([P, 2, P], F32, name=f"spread{q}", tag=f"bank{2 + q}")
+                for i in range(2):
+                    col = 2 * (q % 2) + i
+                    nc.tensor.transpose(spread[:, i, :], columns[:, col : col + 1].to_broadcast([P, P]), ident[:])
+                wide = keep.tile([P, CHUNK], F32, name=f"ts_wide{q}")
+                nc.scalar.copy(out=wide[:], in_=spread[:].rearrange("m i p -> m (i p)"))
+                ts_wide.append(wide[:])
+
+        columns0 = turn_ts(0)
+        nc.scalar.copy(out=bias, in_=bias_turned[:, P - HALVES : P])
+        columns1 = turn_ts(1)
+        spread_ts(0, columns0)
+        spread_ts(1, columns1)
+        quantise_c(1, round_c(1))
+        c_raw.append(load_c(2, C2_AT))
+        c_raw.append(load_c(3, C3_AT))
+
+        sums = {}
+        picked_words = {}
+
+        def open_sums(q):
             for h in range(HALVES):
-                acc = psum.tile([P, CHUNK], F32, name=f"acc{q}{h}", tag=f"bank{SUM_BANKS[q] + h}")
-                for k0 in range(0, CHUNK, P):
-                    cols = slice(q * CHUNK + k0, q * CHUNK + k0 + P)
-                    nc.tensor.matmul_mx(
-                        out=acc[:, k0 : k0 + P],
-                        lhsT=w4_codes[:, 2 * P * h : 2 * P * (h + 1)].bitcast(FP4X4),
-                        lhsT_scale=w4_plane[:, P * h : P * (h + 1)],
-                        rhs=picked_words[:, cols].bitcast(FP8X4),
-                        rhs_scale=picked_scales[:, cols],
-                        start=(k0 == 0),
-                        stop=False,
-                    )
-                sums.append(acc)
+                sums[q, h] = psum.tile([P, CHUNK], F32, name=f"acc{q}{h}", tag=f"bank{SUM_BANKS[q] + h}")
+
+        def pick_words(q):
+            picked = placed.tile([P, CHUNK], U32, name=f"picked_words{q}", align_bytes=64, offset=(C3_AT if q == 3 else PICKED_AT + 4 * CHUNK * (q % 2)))
+            nc.vector.tensor_copy(picked[:], table_words[:].bitcast(U32).indirect(offsets[:, q * CHUNK // 16 : (q + 1) * CHUNK // 16]))
+            picked_words[q] = picked
+
+        def table_passes(q, opens):
+            for h in range(HALVES):
+                nc.tensor.matmul_mx(
+                    out=sums[q, h][:],
+                    lhsT=w4_codes[:, 2 * P * h : 2 * P * (h + 1)].bitcast(FP4X4),
+                    lhsT_scale=w4_plane[:, P * h : P * (h + 1)],
+                    rhs=picked_words[q][:].bitcast(FP8X4),
+                    rhs_scale=picked_scales[:, q * CHUNK : (q + 1) * CHUNK],
+                    start=opens,
+                    stop=not opens,
+                )
+
+        def c_passes(q, opens):
+            for h in range(HALVES):
+                nc.tensor.matmul_mx(
+                    out=sums[q, h][:],
+                    lhsT=first_codes[:, P * h : P * (h + 1)].bitcast(FP8X4),
+                    lhsT_scale=first_plane[:, P * h : P * (h + 1)],
+                    rhs=c_codes[q].bitcast(FP8X4),
+                    rhs_scale=c_planes[q],
+                    start=opens,
+                    stop=not opens,
+                )
 
         def finish(q):
             for h in range(HALVES):
-                nc.tensor.matmul_mx(
-                    out=sums[q * HALVES + h][:],
-                    lhsT=u_codes[:, P * h : P * (h + 1)].bitcast(FP8X4),
-                    lhsT_scale=u_plane[:, P * h : P * (h + 1)],
-                    rhs=c_codes[q][:].bitcast(FP8X4),
-                    rhs_scale=c_planes[q][:],
-                    start=False,
-                    stop=True,
-                )
-            if q == 2:
-                scaled = rest[:, behind_last : behind_last + 2 * CHUNK].rearrange("p (h j) -> p h j", h=HALVES)
-            elif q < 2:
-                scaled = rest[:, q * PACK * CHUNK : (q * PACK + 2) * CHUNK].rearrange("p (h j) -> p h j", h=HALVES)
-            else:
-                scaled = keep.tile([P, HALVES, CHUNK], F32, name="scaled_last")
-            for h in range(HALVES):
                 n = q * HALVES + h
-                if 1 <= n <= 3:
-                    result = rest[:, behind_last + (1 + n) * CHUNK : behind_last + (2 + n) * CHUNK]
+                if q == 2:
+                    scaled = placed.tile([P, CHUNK], F32, name=f"scaled{n}", offset=C3_AT + 4 * CHUNK * (1 + h))
                 else:
-                    result = keep.tile([P, CHUNK], F32, name=f"result{n}")[:]
-                nc.vector.tensor_tensor(scaled[:, h, :], picked_ts[q], sums[n][:], MULT)
-                if n == 0:
-                    nc.gpsimd.tensor_scalar(result, scaled[:, h, :], 1.0, bias[:, h : h + 1], MULT, ADD)
+                    scaled = keep.tile([P, CHUNK], F32, name=f"scaled{n}")
+                if n < 4:
+                    result = placed.tile([P, CHUNK], F32, name=f"result{n}", offset=RESULTS_AT + 4 * CHUNK * n)
                 else:
-                    nc.scalar.activation(result, scaled[:, h, :], IDENT, bias=bias[:, h : h + 1])
+                    result = keep.tile([P, CHUNK], F32, name=f"result{n}")
+                nc.vector.tensor_tensor(scaled[:], ts_wide[q], sums[q, h][:], MULT)
+                nc.scalar.activation(result[:], scaled[:], IDENT, bias=bias[:, h : h + 1])
                 queue = nc.scalar if n == CHUNKS * HALVES - 1 else nc.sync
-                queue.dma_start(out=out[h * P : (h + 1) * P, q * CHUNK : (q + 1) * CHUNK], in_=result)
+                queue.dma_start(out=out[h * P : (h + 1) * P, q * CHUNK : (q + 1) * CHUNK], in_=result[:])
 
-        table_passes(0)
+        open_sums(0)
+        c_passes(0, True)
+        pick_words(0)
+        table_passes(0, False)
+        open_sums(1)
+        pick_words(1)
+        table_passes(1, True)
+        c_passes(1, False)
+        grouped2 = round_c(2)
+        grouped3 = round_c(3)
         finish(0)
-        pick_ts(3, 1, rest[:, 2 * CHUNK : 3 * CHUNK])
-        table_passes(1)
-        table_passes(2)
+        pick_words(2)
+        open_sums(2)
+        table_passes(2, True)
+        quantise_c(2, grouped2)
+        c_passes(2, False)
         finish(1)
-        table_passes(LAST)
+        pick_words(3)
+        open_sums(3)
+        table_passes(3, True)
+        quantise_c(3, grouped3)
+        c_passes(3, False)
         finish(2)
-        finish(LAST)
+        finish(3)

@@ -14,6 +14,7 @@ U8 = mybir.dt.uint8
 FP8X4 = mybir.dt.float8_e4m3fn_x4
 FP4X4 = mybir.dt.float4_e2m1fn_x4
 MULT = mybir.AluOpType.mult
+ADD = mybir.AluOpType.add
 IDENT = mybir.ActivationFunctionType.Identity
 
 P = 128
@@ -28,8 +29,7 @@ COLUMNS_AT = 0
 C0_AT = COLUMNS_AT + RAW // 2
 C2_AT = C0_AT + RAW + 64
 C3_AT = C2_AT + RAW
-RESULTS_AT = C3_AT + RAW
-GATE_AT = RESULTS_AT + RAW
+GATE_AT = C3_AT + RAW
 C1_AT = GATE_AT + 4 * P
 WORDS_AT = C1_AT + RAW
 W4_AT = WORDS_AT + 4 * T
@@ -37,7 +37,7 @@ W4_PLANE_AT = W4_AT + 2 * M
 GATE_END = W4_PLANE_AT + M
 PICKED_AT = GATE_END
 SUM_BANKS = (2, 4, 6, 0)
-CLEAR_SPLIT = 1256
+CLEAR_SPLIT = 1536
 
 
 def load_scale_rows(nc, plane, rows):
@@ -71,7 +71,7 @@ def tile_list_tabts_bias_kernel(tc, tab_words, tab_scales, w4_words, w4_scales, 
         c_rows = c.rearrange("(p t) j -> p t j", t=PACK)
 
         def load_c(q, at):
-            rim = {0: (RAW + 96) // 4, 3: RAW // 4}.get(q, 0)
+            rim = (RAW + 96) // 4 if q == 0 else 0
             tile = placed.tile([P, PACK * CHUNK + rim], F32, name=f"c_raw{q}", offset=at)
             raw = tile[:, 0 : PACK * CHUNK].rearrange("p (t j) -> p t j", t=PACK)
             nc.sync.dma_start(out=raw, in_=c_rows[:, :, q * CHUNK : (q + 1) * CHUNK])
@@ -91,8 +91,7 @@ def tile_list_tabts_bias_kernel(tc, tab_words, tab_scales, w4_words, w4_scales, 
             out=ident[:], in_=zeros, pattern=[[-1, P]], compare_op=mybir.AluOpType.not_equal,
             fill=1.0, base=0, channel_multiplier=1,
         )
-        nc.vector.memset(ts_window[0 : P - 1, 0 : CLEAR_SPLIT - 7], 0.0)
-        nc.vector.memset(ts_window[0 : P - 1, CLEAR_SPLIT - 7 : CLEAR_SPLIT], 0.0)
+        nc.vector.memset(ts_window[0 : P - 1, 0:CLEAR_SPLIT], 0.0)
         nc.gpsimd.memset(ts_window[0 : P - 1, CLEAR_SPLIT:T], 0.0)
 
 
@@ -217,12 +216,12 @@ def tile_list_tabts_bias_kernel(tc, tab_words, tab_scales, w4_words, w4_scales, 
                     scaled = placed.tile([P, CHUNK], F32, name=f"scaled{n}", offset=C3_AT + 4 * CHUNK * (1 + h))
                 else:
                     scaled = keep.tile([P, CHUNK], F32, name=f"scaled{n}")
-                if n < 4:
-                    result = placed.tile([P, CHUNK], F32, name=f"result{n}", offset=RESULTS_AT + 4 * CHUNK * n)
-                else:
-                    result = keep.tile([P, CHUNK], F32, name=f"result{n}")
+                result = keep.tile([P, CHUNK], F32, name=f"result{n}")
                 nc.vector.tensor_tensor(scaled[:], ts_wide[q], sums[q, h][:], MULT)
-                nc.scalar.activation(result[:], scaled[:], IDENT, bias=bias[:, h : h + 1])
+                if q < 2:
+                    nc.gpsimd.tensor_scalar(result[:], scaled[:], 1.0, bias[:, h : h + 1], MULT, ADD)
+                else:
+                    nc.scalar.activation(result[:], scaled[:], IDENT, bias=bias[:, h : h + 1])
                 queue = nc.scalar if n == CHUNKS * HALVES - 1 else nc.sync
                 queue.dma_start(out=out[h * P : (h + 1) * P, q * CHUNK : (q + 1) * CHUNK], in_=result[:])
 

@@ -29,7 +29,8 @@ COLUMNS_AT = 0
 C0_AT = COLUMNS_AT + RAW // 2
 C2_AT = C0_AT + RAW + 64
 C3_AT = C2_AT + RAW
-GATE_AT = C3_AT + RAW
+RESULTS_AT = C3_AT + RAW
+GATE_AT = RESULTS_AT + RAW // 2
 C1_AT = GATE_AT + 4 * P
 WORDS_AT = C1_AT + RAW
 W4_AT = WORDS_AT + 4 * T
@@ -38,11 +39,12 @@ GATE_END = W4_PLANE_AT + M
 PICKED_AT = GATE_END
 SUM_BANKS = (2, 4, 6, 0)
 CLEAR_SPLIT = 1536
+SHARE = 64
 
 
 def load_scale_rows(nc, plane, rows):
-    for q in range(4):
-        nc.sync.dma_start(out=plane[32 * q : 32 * q + 4, :].bitcast(I32), in_=rows[4 * q : 4 * q + 4, :].bitcast(I32))
+    for r in range(4):
+        nc.sync.dma_start(out=plane[r:P:32, :].bitcast(I32), in_=rows[r:16:4, :].bitcast(I32))
 
 
 def interleave(nc, grouped, raw):
@@ -71,7 +73,7 @@ def tile_list_tabts_bias_kernel(tc, tab_words, tab_scales, w4_words, w4_scales, 
         c_rows = c.rearrange("(p t) j -> p t j", t=PACK)
 
         def load_c(q, at):
-            rim = (RAW + 96) // 4 if q == 0 else 0
+            rim = {0: (RAW + 96) // 4, 3: RAW // 8}.get(q, 0)
             tile = placed.tile([P, PACK * CHUNK + rim], F32, name=f"c_raw{q}", offset=at)
             raw = tile[:, 0 : PACK * CHUNK].rearrange("p (t j) -> p t j", t=PACK)
             nc.sync.dma_start(out=raw, in_=c_rows[:, :, q * CHUNK : (q + 1) * CHUNK])
@@ -129,11 +131,17 @@ def tile_list_tabts_bias_kernel(tc, tab_words, tab_scales, w4_words, w4_scales, 
 
         def round_c(q):
             grouped = placed.tile([P, CHUNK, PACK], BF16, name=f"c_grouped{q}", align_bytes=64, offset=COLUMNS_AT + (q - 1) * RAW // 2)
-            interleave(nc, grouped[:], c_raw[q])
+            cut = CHUNK - SHARE if q == CHUNKS - 1 else CHUNK
+            interleave(nc, grouped[:, 0:cut, :], c_raw[q][:, :, 0:cut])
+            if cut < CHUNK:
+                nc.gpsimd.tensor_scalar(grouped[:, cut:CHUNK, :], c_raw[q][:, :, cut:CHUNK].rearrange("p t j -> p j t"), 1.0, 0.0, MULT, ADD)
             return grouped
 
         def quantise_c(q, grouped):
-            codes = keep.tile([P, CHUNK], U32, name=f"c_codes{q}", align_bytes=64)
+            if q == 1:
+                codes = placed.tile([P, CHUNK], U32, name="c_codes1", align_bytes=64, offset=PICKED_AT + 4 * CHUNK)
+            else:
+                codes = keep.tile([P, CHUNK], U32, name=f"c_codes{q}", align_bytes=64)
             plane = keep.tile([P, CHUNK], U8, name=f"c_plane{q}", align_bytes=64)
             nc.vector.quantize_mx(out=codes[:].bitcast(FP8X4), scales=plane[:], in_=grouped[:].rearrange("p j t -> p (j t)"))
             c_codes.append(codes[:])
@@ -169,7 +177,7 @@ def tile_list_tabts_bias_kernel(tc, tab_words, tab_scales, w4_words, w4_scales, 
         columns1 = turn_ts(1)
         spread_ts(0, columns0)
         spread_ts(1, columns1)
-        quantise_c(1, round_c(1))
+        grouped1 = round_c(1)
         c_raw.append(load_c(2, C2_AT))
         c_raw.append(load_c(3, C3_AT))
 
@@ -181,8 +189,9 @@ def tile_list_tabts_bias_kernel(tc, tab_words, tab_scales, w4_words, w4_scales, 
                 sums[q, h] = psum.tile([P, CHUNK], F32, name=f"acc{q}{h}", tag=f"bank{SUM_BANKS[q] + h}")
 
         def pick_words(q):
-            picked = placed.tile([P, CHUNK], U32, name=f"picked_words{q}", align_bytes=64, offset=(C3_AT if q == 3 else PICKED_AT + 4 * CHUNK * (q % 2)))
-            nc.vector.tensor_copy(picked[:], table_words[:].bitcast(U32).indirect(offsets[:, q * CHUNK // 16 : (q + 1) * CHUNK // 16]))
+            width = 2 * CHUNK if q == 0 else CHUNK
+            picked = placed.tile([P, width], U32, name=f"picked_words{q}", align_bytes=64, offset=PICKED_AT + 8 * CHUNK * (q % 2))[:, 0:CHUNK]
+            nc.vector.tensor_copy(picked, table_words[:].bitcast(U32).indirect(offsets[:, q * CHUNK // 16 : (q + 1) * CHUNK // 16]))
             picked_words[q] = picked
 
         def table_passes(q, opens):
@@ -191,7 +200,7 @@ def tile_list_tabts_bias_kernel(tc, tab_words, tab_scales, w4_words, w4_scales, 
                     out=sums[q, h][:],
                     lhsT=w4_codes[:, 2 * P * h : 2 * P * (h + 1)].bitcast(FP4X4),
                     lhsT_scale=w4_plane[:, P * h : P * (h + 1)],
-                    rhs=picked_words[q][:].bitcast(FP8X4),
+                    rhs=picked_words[q].bitcast(FP8X4),
                     rhs_scale=picked_scales[:, q * CHUNK : (q + 1) * CHUNK],
                     start=opens,
                     stop=not opens,
@@ -216,9 +225,12 @@ def tile_list_tabts_bias_kernel(tc, tab_words, tab_scales, w4_words, w4_scales, 
                     scaled = placed.tile([P, CHUNK], F32, name=f"scaled{n}", offset=C3_AT + 4 * CHUNK * (1 + h))
                 else:
                     scaled = keep.tile([P, CHUNK], F32, name=f"scaled{n}")
-                result = keep.tile([P, CHUNK], F32, name=f"result{n}")
+                if q == 1:
+                    result = placed.tile([P, CHUNK], F32, name=f"result{n}", offset=RESULTS_AT + 4 * CHUNK * h)
+                else:
+                    result = keep.tile([P, CHUNK], F32, name=f"result{n}")
                 nc.vector.tensor_tensor(scaled[:], ts_wide[q], sums[q, h][:], MULT)
-                if q < 2:
+                if q == 0:
                     nc.gpsimd.tensor_scalar(result[:], scaled[:], 1.0, bias[:, h : h + 1], MULT, ADD)
                 else:
                     nc.scalar.activation(result[:], scaled[:], IDENT, bias=bias[:, h : h + 1])
@@ -232,19 +244,20 @@ def tile_list_tabts_bias_kernel(tc, tab_words, tab_scales, w4_words, w4_scales, 
         open_sums(1)
         pick_words(1)
         table_passes(1, True)
-        c_passes(1, False)
         grouped2 = round_c(2)
         grouped3 = round_c(3)
         finish(0)
         pick_words(2)
+        quantise_c(1, grouped1)
+        c_passes(1, False)
         open_sums(2)
         table_passes(2, True)
-        quantise_c(2, grouped2)
-        c_passes(2, False)
-        finish(1)
         pick_words(3)
         open_sums(3)
         table_passes(3, True)
+        finish(1)
+        quantise_c(2, grouped2)
+        c_passes(2, False)
         quantise_c(3, grouped3)
         c_passes(3, False)
         finish(2)

@@ -79,14 +79,12 @@ def tile_list_tabts_bias_kernel(tc, tab_words, tab_scales, w4_words, w4_scales, 
             nc.sync.dma_start(out=raw, in_=c_rows[:, :, q * CHUNK : (q + 1) * CHUNK])
             return raw
 
-        c_raw = [load_c(0, C0_AT)]
-
         table_scales = keep.tile([P, T], U8, name="table_scales", align_bytes=64)
         nc.vector.memset(table_scales[:].bitcast(I32), 0)
         load_scale_rows(nc, table_scales, tab_scales[0])
 
-        gate = placed.tile([P, (GATE_END - GATE_AT) // 4], F32, name="gate", offset=GATE_AT)
-        zeros = gate[:, 0:P]
+        gate = placed.tile([P, (GATE_END - C0_AT) // 4], F32, name="gate", offset=C0_AT)
+        zeros = gate[:, (GATE_AT - C0_AT) // 4 : (GATE_AT - C0_AT) // 4 + P]
         nc.vector.memset(zeros, 0.0)
         ident = keep.tile([P, P], F32, name="ident")
         nc.gpsimd.affine_select(
@@ -96,6 +94,8 @@ def tile_list_tabts_bias_kernel(tc, tab_words, tab_scales, w4_words, w4_scales, 
         nc.vector.memset(ts_window[0 : P - 1, 0:CLEAR_SPLIT], 0.0)
         nc.gpsimd.memset(ts_window[0 : P - 1, CLEAR_SPLIT:T], 0.0)
 
+
+        c_raw = [load_c(0, C0_AT)]
 
         table_words = placed.tile([P, T], I32, name="table_words", align_bytes=64, offset=WORDS_AT)
         nc.sync.dma_start(out=table_words[:], in_=tab_words[0].rearrange("p t i -> p (t i)").bitcast(I32))

@@ -22,21 +22,24 @@ PACK = 4
 HALVES = M // P
 CHUNK = 256
 CHUNKS = S // CHUNK
+LAST = CHUNKS - 1
 BANK = 512
 RAW = 4 * PACK * CHUNK
 
 COLUMNS_AT = 0
 C0_AT = COLUMNS_AT + RAW // 2
-C2_AT = C0_AT + RAW + 64
+WIDE_AT = C0_AT + RAW
+C2_AT = WIDE_AT + RAW // 2 + 64
 C3_AT = C2_AT + RAW
 RESULTS_AT = C3_AT + RAW
-GATE_AT = RESULTS_AT + RAW // 2
+GATE_AT = RESULTS_AT + RAW
 C1_AT = GATE_AT + 4 * P
 WORDS_AT = C1_AT + RAW
 W4_AT = WORDS_AT + 4 * T
 W4_PLANE_AT = W4_AT + 2 * M
 GATE_END = W4_PLANE_AT + M
 PICKED_AT = GATE_END
+U_AT = PICKED_AT + 4 * 4 * CHUNK
 SUM_BANKS = (2, 4, 6, 0)
 CLEAR_SPLIT = 1536
 SHARE = 64
@@ -67,13 +70,13 @@ def tile_list_tabts_bias_kernel(tc, tab_words, tab_scales, w4_words, w4_scales, 
         ts_window = keep.tile([P, T], F32, name="ts_window")
         nc.sync.dma_start(out=ts_window[P - 1 : P, :], in_=ts[0:1, :])
 
-        u_raw = keep.tile([P, PACK, M], F32, name="u_raw")[:]
+        u_raw = placed.tile([P, PACK, M], F32, name="u_raw", offset=U_AT)[:]
         nc.sync.dma_start(out=u_raw, in_=u.rearrange("(p t) n -> p t n", t=PACK))
 
         c_rows = c.rearrange("(p t) j -> p t j", t=PACK)
 
         def load_c(q, at):
-            rim = {0: (RAW + 96) // 4, 3: RAW // 8}.get(q, 0)
+            rim = {0: (RAW // 2 + 64) // 4, 3: RAW // 4}.get(q, 0)
             tile = placed.tile([P, PACK * CHUNK + rim], F32, name=f"c_raw{q}", offset=at)
             raw = tile[:, 0 : PACK * CHUNK].rearrange("p (t j) -> p t j", t=PACK)
             nc.sync.dma_start(out=raw, in_=c_rows[:, :, q * CHUNK : (q + 1) * CHUNK])
@@ -122,24 +125,25 @@ def tile_list_tabts_bias_kernel(tc, tab_words, tab_scales, w4_words, w4_scales, 
 
         first = keep.tile([P, M + CHUNK, PACK], BF16, name="first", align_bytes=64)
         interleave(nc, first[:, 0:M, :], u_raw)
-        interleave(nc, first[:, M : M + CHUNK, :], c_raw[0])
         first_codes = keep.tile([P, M + CHUNK], U32, name="first_codes", align_bytes=64)
         first_plane = keep.tile([P, M + CHUNK], U8, name="first_plane", align_bytes=64)
-        nc.vector.quantize_mx(out=first_codes[:].bitcast(FP8X4), scales=first_plane[:], in_=first[:].rearrange("p n t -> p (n t)"))
         c_codes = [first_codes[:, M : M + CHUNK]]
         c_planes = [first_plane[:, M : M + CHUNK]]
 
         def round_c(q):
             grouped = placed.tile([P, CHUNK, PACK], BF16, name=f"c_grouped{q}", align_bytes=64, offset=COLUMNS_AT + (q - 1) * RAW // 2)
-            cut = CHUNK - SHARE if q == CHUNKS - 1 else CHUNK
-            interleave(nc, grouped[:, 0:cut, :], c_raw[q][:, :, 0:cut])
-            if cut < CHUNK:
+            if q < LAST:
+                interleave(nc, grouped[:], c_raw[q])
+            else:
+                cut = CHUNK - SHARE
+                interleave(nc, grouped[:, 0:P, :], c_raw[q][:, :, 0:P])
+                interleave(nc, grouped[:, P:cut, :], c_raw[q][:, :, P:cut])
                 nc.gpsimd.tensor_scalar(grouped[:, cut:CHUNK, :], c_raw[q][:, :, cut:CHUNK].rearrange("p t j -> p j t"), 1.0, 0.0, MULT, ADD)
             return grouped
 
         def quantise_c(q, grouped):
             if q == 1:
-                codes = placed.tile([P, CHUNK], U32, name="c_codes1", align_bytes=64, offset=PICKED_AT + 4 * CHUNK)
+                codes = placed.tile([P, CHUNK], U32, name="c_codes1", align_bytes=64, offset=PICKED_AT + 3 * 4 * CHUNK)
             else:
                 codes = keep.tile([P, CHUNK], U32, name=f"c_codes{q}", align_bytes=64)
             plane = keep.tile([P, CHUNK], U8, name=f"c_plane{q}", align_bytes=64)
@@ -149,16 +153,17 @@ def tile_list_tabts_bias_kernel(tc, tab_words, tab_scales, w4_words, w4_scales, 
 
         bias_turned = psum.tile([P, P], F32, name="bias_turned", tag="bank7")
         nc.tensor.transpose(bias_turned[:], bias_rows[:], ident[:])
-        bias = placed.tile([P, HALVES], F32, name="bias", offset=C2_AT - 32)[:]
 
         ts_wide = []
-        ts_columns = placed.tile([P, (RAW + 32) // 4], F32, name="ts_columns", offset=COLUMNS_AT)
 
         def turn_ts(g):
             turned = psum.tile([P, 4, P], F32, name=f"turned{g}", tag=f"bank{g}")
             for i in range(4):
                 nc.tensor.transpose(turned[:, i, :], picked_ts[g][:, i * P : (i + 1) * P], ident[:])
-            columns = ts_columns[:, 8 * g : 8 * g + 4]
+            if g == 0:
+                columns = placed.tile([P, 4], F32, name="columns0", offset=U_AT)[:]
+            else:
+                columns = placed.tile([P, (RAW + 32) // 4], F32, name="columns1", offset=COLUMNS_AT)[:, 0:4]
             nc.scalar.copy(out=columns, in_=turned[:, :, P - 1])
             return columns
 
@@ -168,14 +173,20 @@ def tile_list_tabts_bias_kernel(tc, tab_words, tab_scales, w4_words, w4_scales, 
                 for i in range(2):
                     col = 2 * (q % 2) + i
                     nc.tensor.transpose(spread[:, i, :], columns[:, col : col + 1].to_broadcast([P, P]), ident[:])
-                wide = keep.tile([P, CHUNK], F32, name=f"ts_wide{q}")
+                if g == 0:
+                    wide = placed.tile([P, CHUNK], F32, name=f"ts_wide{q}", offset=WIDE_AT + 4 * CHUNK * q)
+                else:
+                    wide = keep.tile([P, CHUNK], F32, name=f"ts_wide{q}")
                 nc.scalar.copy(out=wide[:], in_=spread[:].rearrange("m i p -> m (i p)"))
                 ts_wide.append(wide[:])
 
         columns0 = turn_ts(0)
-        nc.scalar.copy(out=bias, in_=bias_turned[:, P - HALVES : P])
+        interleave(nc, first[:, M : M + CHUNK, :], c_raw[0])
+        nc.vector.quantize_mx(out=first_codes[:].bitcast(FP8X4), scales=first_plane[:], in_=first[:].rearrange("p n t -> p (n t)"))
         columns1 = turn_ts(1)
         spread_ts(0, columns0)
+        bias = placed.tile([P, HALVES], F32, name="bias", offset=C2_AT - 32)[:]
+        nc.scalar.copy(out=bias, in_=bias_turned[:, P - HALVES : P])
         spread_ts(1, columns1)
         grouped1 = round_c(1)
         c_raw.append(load_c(2, C2_AT))
@@ -189,8 +200,7 @@ def tile_list_tabts_bias_kernel(tc, tab_words, tab_scales, w4_words, w4_scales, 
                 sums[q, h] = psum.tile([P, CHUNK], F32, name=f"acc{q}{h}", tag=f"bank{SUM_BANKS[q] + h}")
 
         def pick_words(q):
-            width = 2 * CHUNK if q == 0 else CHUNK
-            picked = placed.tile([P, width], U32, name=f"picked_words{q}", align_bytes=64, offset=PICKED_AT + 8 * CHUNK * (q % 2))[:, 0:CHUNK]
+            picked = placed.tile([P, 2 * CHUNK if q == 0 else CHUNK], U32, name=f"picked_words{q}", align_bytes=64, offset=PICKED_AT + 4 * CHUNK * (2, 0, 1, 2)[q])[:, 0:CHUNK]
             nc.vector.tensor_copy(picked, table_words[:].bitcast(U32).indirect(offsets[:, q * CHUNK // 16 : (q + 1) * CHUNK // 16]))
             picked_words[q] = picked
 
@@ -225,17 +235,16 @@ def tile_list_tabts_bias_kernel(tc, tab_words, tab_scales, w4_words, w4_scales, 
                     scaled = placed.tile([P, CHUNK], F32, name=f"scaled{n}", offset=C3_AT + 4 * CHUNK * (1 + h))
                 else:
                     scaled = keep.tile([P, CHUNK], F32, name=f"scaled{n}")
-                if q == 1:
-                    result = placed.tile([P, CHUNK], F32, name=f"result{n}", offset=RESULTS_AT + 4 * CHUNK * h)
+                if 1 <= n <= 3:
+                    result = placed.tile([P, CHUNK], F32, name=f"result{n}", offset=RESULTS_AT + 4 * CHUNK * (n - 1))
                 else:
                     result = keep.tile([P, CHUNK], F32, name=f"result{n}")
                 nc.vector.tensor_tensor(scaled[:], ts_wide[q], sums[q, h][:], MULT)
-                if q == 0:
+                if n == 0:
                     nc.gpsimd.tensor_scalar(result[:], scaled[:], 1.0, bias[:, h : h + 1], MULT, ADD)
                 else:
                     nc.scalar.activation(result[:], scaled[:], IDENT, bias=bias[:, h : h + 1])
-                queue = nc.scalar if n == CHUNKS * HALVES - 1 else nc.sync
-                queue.dma_start(out=out[h * P : (h + 1) * P, q * CHUNK : (q + 1) * CHUNK], in_=result[:])
+                nc.sync.dma_start(out=out[h * P : (h + 1) * P, q * CHUNK : (q + 1) * CHUNK], in_=result[:])
 
         open_sums(0)
         c_passes(0, True)
@@ -244,21 +253,53 @@ def tile_list_tabts_bias_kernel(tc, tab_words, tab_scales, w4_words, w4_scales, 
         open_sums(1)
         pick_words(1)
         table_passes(1, True)
+        pick_words(2)
         grouped2 = round_c(2)
         grouped3 = round_c(3)
         finish(0)
-        pick_words(2)
         quantise_c(1, grouped1)
         c_passes(1, False)
         open_sums(2)
         table_passes(2, True)
         pick_words(3)
-        open_sums(3)
-        table_passes(3, True)
+        last_sums = []
+        for k in range(2):
+            acc = psum.tile([P, HALVES, P], F32, name=f"last_acc{k}", tag=f"bank{SUM_BANKS[LAST] + k}")
+            for h in range(HALVES):
+                nc.tensor.matmul_mx(
+                    out=acc[:, h, :],
+                    lhsT=w4_codes[:, 2 * P * h : 2 * P * (h + 1)].bitcast(FP4X4),
+                    lhsT_scale=w4_plane[:, P * h : P * (h + 1)],
+                    rhs=picked_words[LAST][:, k * P : (k + 1) * P].bitcast(FP8X4),
+                    rhs_scale=picked_scales[:, LAST * CHUNK + k * P : LAST * CHUNK + (k + 1) * P],
+                    start=(h == 0),
+                    stop=False,
+                )
+            last_sums.append(acc)
         finish(1)
         quantise_c(2, grouped2)
         c_passes(2, False)
-        quantise_c(3, grouped3)
-        c_passes(3, False)
+        for k in range(2):
+            codes = keep.tile([P, P], U32, name=f"last_codes{k}", align_bytes=64)
+            plane = keep.tile([P, P], U8, name=f"last_plane{k}", align_bytes=64)
+            nc.vector.quantize_mx(out=codes[:].bitcast(FP8X4), scales=plane[:], in_=grouped3[:, k * P : (k + 1) * P, :].rearrange("p j t -> p (j t)"))
+            for h in range(HALVES):
+                nc.tensor.matmul_mx(
+                    out=last_sums[k][:, h, :],
+                    lhsT=first_codes[:, P * h : P * (h + 1)].bitcast(FP8X4),
+                    lhsT_scale=first_plane[:, P * h : P * (h + 1)],
+                    rhs=codes[:].bitcast(FP8X4),
+                    rhs_scale=plane[:],
+                    start=False,
+                    stop=(h == HALVES - 1),
+                )
         finish(2)
-        finish(3)
+        last_result = keep.tile([P, HALVES, CHUNK], F32, name="last_result")
+        for k in range(2):
+            scaled = keep.tile([P, HALVES, P], F32, name=f"last_scaled{k}")
+            wide = ts_wide[LAST][:, k * P : (k + 1) * P].unsqueeze(1).to_broadcast([P, HALVES, P])
+            nc.vector.tensor_tensor(scaled[:], wide, last_sums[k][:], MULT)
+            for h in range(HALVES):
+                nc.scalar.activation(last_result[:, h, k * P : (k + 1) * P], scaled[:, h, :], IDENT, bias=bias[:, h : h + 1])
+        for h, queue in enumerate((nc.sync, nc.scalar)):
+            queue.dma_start(out=out[h * P : (h + 1) * P, LAST * CHUNK : S], in_=last_result[:, h, :])

@@ -37,11 +37,11 @@ C1_AT = GATE_AT + 4 * P
 WORDS_AT = C1_AT + RAW
 W4_AT = WORDS_AT + 4 * T
 W4_PLANE_AT = W4_AT + 2 * M
-GATE_END = W4_PLANE_AT + M
+BIAS_ROWS_AT = W4_PLANE_AT + M
+GATE_END = BIAS_ROWS_AT + 4 * P
 PICKED_AT = GATE_END
 U_AT = PICKED_AT + 4 * 4 * CHUNK
 SUM_BANKS = (2, 4, 6, 0)
-CLEAR_SPLIT = 1536
 SHARE = 64
 
 
@@ -94,11 +94,14 @@ def tile_list_tabts_bias_kernel(tc, tab_words, tab_scales, w4_words, w4_scales, 
             out=ident[:], in_=zeros, pattern=[[-1, P]], compare_op=mybir.AluOpType.not_equal,
             fill=1.0, base=0, channel_multiplier=1,
         )
-        nc.vector.memset(ts_window[0 : P - 1, 0:CLEAR_SPLIT], 0.0)
-        nc.gpsimd.memset(ts_window[0 : P - 1, CLEAR_SPLIT:T], 0.0)
+        for half in range(2):
+            nc.vector.memset(ts_window[0 : P - 1, half * T // 2 : (half + 1) * T // 2], 0.0)
 
 
         c_raw = [load_c(0, C0_AT)]
+
+        bias_rows = placed.tile([P, P], F32, name="bias_rows", offset=BIAS_ROWS_AT)
+        nc.sync.dma_start(out=bias_rows[P - HALVES : P, :], in_=b.rearrange("(h p) -> h p", p=P))
 
         table_words = placed.tile([P, T], I32, name="table_words", align_bytes=64, offset=WORDS_AT)
         nc.sync.dma_start(out=table_words[:], in_=tab_words[0].rearrange("p t i -> p (t i)").bitcast(I32))
@@ -110,21 +113,19 @@ def tile_list_tabts_bias_kernel(tc, tab_words, tab_scales, w4_words, w4_scales, 
         w4_plane = placed.tile([P, M], U8, name="w4_plane", align_bytes=64, offset=W4_PLANE_AT)[:]
         nc.gpsimd.memset(w4_plane.bitcast(I32), 0)
         load_scale_rows(nc, w4_plane, w4_scales[0])
-
-        bias_rows = keep.tile([P, P], F32, name="bias_rows")
         nc.gpsimd.memset(bias_rows[0 : P - HALVES, :], 0.0)
-        nc.sync.dma_start(out=bias_rows[P - HALVES : P, :], in_=b.rearrange("(h p) -> h p", p=P))
+
 
         picked_ts = []
         for g in range(2):
             picked = keep.tile([P, BANK], F32, name=f"picked_ts{g}")
             nc.vector.tensor_copy(picked[:], ts_window[:].indirect(offsets[:, g * BANK // 16 : (g + 1) * BANK // 16]))
             picked_ts.append(picked)
-        picked_scales = keep.tile([P, S], U8, name="picked_scales", align_bytes=64)
-        nc.vector.tensor_copy(picked_scales[:], table_scales[:].indirect(offsets[:]))
-
         first = keep.tile([P, M + CHUNK, PACK], BF16, name="first", align_bytes=64)
         interleave(nc, first[:, 0:M, :], u_raw)
+        picked_scales = placed.tile([P, S], U8, name="picked_scales", align_bytes=64, offset=U_AT + 64)
+        nc.vector.tensor_copy(picked_scales[:], table_scales[:].indirect(offsets[:]))
+
         first_codes = keep.tile([P, M + CHUNK], U32, name="first_codes", align_bytes=64)
         first_plane = keep.tile([P, M + CHUNK], U8, name="first_plane", align_bytes=64)
         c_codes = [first_codes[:, M : M + CHUNK]]

@@ -94,8 +94,10 @@ def tile_list_tabts_bias_kernel(tc, tab_words, tab_scales, w4_words, w4_scales, 
             out=ident[:], in_=zeros, pattern=[[-1, P]], compare_op=mybir.AluOpType.not_equal,
             fill=1.0, base=0, channel_multiplier=1,
         )
-        for half in range(2):
-            nc.vector.memset(ts_window[0 : P - 1, half * T // 2 : (half + 1) * T // 2], 0.0)
+        nc.vector.memset(ts_window[0 : P - 1, 0 : T // 2], 0.0)
+        w4_plane = placed.tile([P, M], U8, name="w4_plane", align_bytes=64, offset=W4_PLANE_AT)[:]
+        nc.vector.memset(w4_plane.bitcast(I32), 0)
+        nc.vector.memset(ts_window[0 : P - 1, T // 2 : T], 0.0)
 
 
         c_raw = [load_c(0, C0_AT)]
@@ -110,10 +112,8 @@ def tile_list_tabts_bias_kernel(tc, tab_words, tab_scales, w4_words, w4_scales, 
 
         w4_codes = placed.tile([P, 2 * M], U8, name="w4_codes", align_bytes=64, offset=W4_AT)[:]
         nc.sync.dma_start(out=w4_codes.bitcast(I32), in_=w4_words[0].bitcast(I32))
-        w4_plane = placed.tile([P, M], U8, name="w4_plane", align_bytes=64, offset=W4_PLANE_AT)[:]
-        nc.gpsimd.memset(w4_plane.bitcast(I32), 0)
         load_scale_rows(nc, w4_plane, w4_scales[0])
-        nc.gpsimd.memset(bias_rows[0 : P - HALVES, :], 0.0)
+        nc.scalar.copy(out=bias_rows[0 : P - HALVES, :], in_=ident[0 : P - HALVES, :])
 
 
         picked_ts = []

@@ -245,7 +245,8 @@ def tile_list_tabts_bias_kernel(tc, tab_words, tab_scales, w4_words, w4_scales, 
                     nc.gpsimd.tensor_scalar(result[:], scaled[:], 1.0, bias[:, h : h + 1], MULT, ADD)
                 else:
                     nc.scalar.activation(result[:], scaled[:], IDENT, bias=bias[:, h : h + 1])
-                nc.sync.dma_start(out=out[h * P : (h + 1) * P, q * CHUNK : (q + 1) * CHUNK], in_=result[:])
+                queue = nc.scalar if n == CHUNKS * HALVES - 1 else nc.sync
+                queue.dma_start(out=out[h * P : (h + 1) * P, q * CHUNK : (q + 1) * CHUNK], in_=result[:])
 
         open_sums(0)
         c_passes(0, True)
@@ -263,20 +264,8 @@ def tile_list_tabts_bias_kernel(tc, tab_words, tab_scales, w4_words, w4_scales, 
         open_sums(2)
         table_passes(2, True)
         pick_words(3)
-        last_sums = []
-        for k in range(2):
-            acc = psum.tile([P, HALVES, P], F32, name=f"last_acc{k}", tag=f"bank{SUM_BANKS[LAST] + k}")
-            for h in range(HALVES):
-                nc.tensor.matmul_mx(
-                    out=acc[:, h, :],
-                    lhsT=w4_codes[:, 2 * P * h : 2 * P * (h + 1)].bitcast(FP4X4),
-                    lhsT_scale=w4_plane[:, P * h : P * (h + 1)],
-                    rhs=picked_words[LAST][:, k * P : (k + 1) * P].bitcast(FP8X4),
-                    rhs_scale=picked_scales[:, LAST * CHUNK + k * P : LAST * CHUNK + (k + 1) * P],
-                    start=(h == 0),
-                    stop=False,
-                )
-            last_sums.append(acc)
+        open_sums(LAST)
+        table_passes(LAST, True)
         finish(1)
         quantise_c(2, grouped2)
         c_passes(2, False)
@@ -286,21 +275,13 @@ def tile_list_tabts_bias_kernel(tc, tab_words, tab_scales, w4_words, w4_scales, 
             nc.vector.quantize_mx(out=codes[:].bitcast(FP8X4), scales=plane[:], in_=grouped3[:, k * P : (k + 1) * P, :].rearrange("p j t -> p (j t)"))
             for h in range(HALVES):
                 nc.tensor.matmul_mx(
-                    out=last_sums[k][:, h, :],
+                    out=sums[LAST, h][:, k * P : (k + 1) * P],
                     lhsT=first_codes[:, P * h : P * (h + 1)].bitcast(FP8X4),
                     lhsT_scale=first_plane[:, P * h : P * (h + 1)],
                     rhs=codes[:].bitcast(FP8X4),
                     rhs_scale=plane[:],
                     start=False,
-                    stop=(h == HALVES - 1),
+                    stop=(k == 1),
                 )
         finish(2)
-        last_result = keep.tile([P, HALVES, CHUNK], F32, name="last_result")
-        for k in range(2):
-            scaled = keep.tile([P, HALVES, P], F32, name=f"last_scaled{k}")
-            wide = ts_wide[LAST][:, k * P : (k + 1) * P].unsqueeze(1).to_broadcast([P, HALVES, P])
-            nc.vector.tensor_tensor(scaled[:], wide, last_sums[k][:], MULT)
-            for h in range(HALVES):
-                nc.scalar.activation(last_result[:, h, k * P : (k + 1) * P], scaled[:, h, :], IDENT, bias=bias[:, h : h + 1])
-        for h, queue in enumerate((nc.sync, nc.scalar)):
-            queue.dma_start(out=out[h * P : (h + 1) * P, LAST * CHUNK : S], in_=last_result[:, h, :])
+        finish(LAST)

@@ -79,7 +79,9 @@ def tile_list_tabts_bias_kernel(tc, tab_words, tab_scales, w4_words, w4_scales, 
             rim = {0: (RAW // 2 + 64) // 4, 3: RAW // 4}.get(q, 0)
             tile = placed.tile([P, PACK * CHUNK + rim], F32, name=f"c_raw{q}", offset=at)
             raw = tile[:, 0 : PACK * CHUNK].rearrange("p (t j) -> p t j", t=PACK)
-            nc.sync.dma_start(out=raw, in_=c_rows[:, :, q * CHUNK : (q + 1) * CHUNK])
+            width = P if q == LAST else CHUNK
+            for j in range(0, CHUNK, width):
+                nc.sync.dma_start(out=raw[:, :, j : j + width], in_=c_rows[:, :, q * CHUNK + j : q * CHUNK + j + width])
             return raw
 
         table_scales = keep.tile([P, T], U8, name="table_scales", align_bytes=64)

@@ -110,10 +110,9 @@ def tile_list_tabts_bias_kernel(tc, tab_words, tab_scales, w4_words, w4_scales, 
         table_words = placed.tile([P, T], I32, name="table_words", align_bytes=64, offset=WORDS_AT)
         nc.sync.dma_start(out=table_words[:], in_=tab_words[0].rearrange("p t i -> p (t i)").bitcast(I32))
 
-        c_raw.append(load_c(1, C1_AT))
-
         w4_codes = placed.tile([P, 2 * M], U8, name="w4_codes", align_bytes=64, offset=W4_AT)[:]
         nc.sync.dma_start(out=w4_codes.bitcast(I32), in_=w4_words[0].bitcast(I32))
+        c_raw.append(load_c(1, C1_AT))
         load_scale_rows(nc, w4_plane, w4_scales[0])
         nc.scalar.copy(out=bias_rows[0 : P - HALVES, :], in_=ident[0 : P - HALVES, :])
 

@@ -29,7 +29,8 @@ RAW = 4 * PACK * CHUNK
 COLUMNS_AT = 0
 C0_AT = COLUMNS_AT + RAW // 2
 WIDE_AT = C0_AT + RAW
-C2_AT = WIDE_AT + RAW // 2 + 64
+LINE = 256
+C2_AT = WIDE_AT + RAW // 2 + LINE
 C3_AT = C2_AT + RAW
 RESULTS_AT = C3_AT + RAW
 GATE_AT = RESULTS_AT + RAW
@@ -67,7 +68,7 @@ def tile_list_tabts_bias_kernel(tc, tab_words, tab_scales, w4_words, w4_scales, 
         offsets = keep.tile([P, S // 16], U16, name="offsets")
         nc.sync.dma_start(offsets[:], offs)
 
-        ts_window = keep.tile([P, T], F32, name="ts_window")
+        ts_window = keep.tile([P, T], F32, name="ts_window", align_bytes=LINE)
         nc.sync.dma_start(out=ts_window[P - 1 : P, :], in_=ts[0:1, :])
 
         u_raw = placed.tile([P, PACK, M], F32, name="u_raw", offset=U_AT)[:]
@@ -76,7 +77,7 @@ def tile_list_tabts_bias_kernel(tc, tab_words, tab_scales, w4_words, w4_scales, 
         c_rows = c.rearrange("(p t) j -> p t j", t=PACK)
 
         def load_c(q, at):
-            rim = {0: (RAW // 2 + 64) // 4, 3: RAW // 4}.get(q, 0)
+            rim = {0: (RAW // 2 + LINE) // 4, 3: RAW // 4}.get(q, 0)
             tile = placed.tile([P, PACK * CHUNK + rim], F32, name=f"c_raw{q}", offset=at)
             raw = tile[:, 0 : PACK * CHUNK].rearrange("p (t j) -> p t j", t=PACK)
             width = P if q == LAST else CHUNK
@@ -84,7 +85,7 @@ def tile_list_tabts_bias_kernel(tc, tab_words, tab_scales, w4_words, w4_scales, 
                 nc.sync.dma_start(out=raw[:, :, j : j + width], in_=c_rows[:, :, q * CHUNK + j : q * CHUNK + j + width])
             return raw
 
-        table_scales = keep.tile([P, T], U8, name="table_scales", align_bytes=64)
+        table_scales = keep.tile([P, T], U8, name="table_scales", align_bytes=LINE)
         nc.vector.memset(table_scales[:].bitcast(I32), 0)
         load_scale_rows(nc, table_scales, tab_scales[0])
 
@@ -107,7 +108,7 @@ def tile_list_tabts_bias_kernel(tc, tab_words, tab_scales, w4_words, w4_scales, 
         bias_rows = placed.tile([P, P], F32, name="bias_rows", offset=BIAS_ROWS_AT)
         nc.sync.dma_start(out=bias_rows[P - HALVES : P, :], in_=b.rearrange("(h p) -> h p", p=P))
 
-        table_words = placed.tile([P, T], I32, name="table_words", align_bytes=64, offset=WORDS_AT)
+        table_words = placed.tile([P, T], I32, name="table_words", align_bytes=LINE, offset=WORDS_AT)
         nc.sync.dma_start(out=table_words[:], in_=tab_words[0].rearrange("p t i -> p (t i)").bitcast(I32))
 
         w4_codes = placed.tile([P, 2 * M], U8, name="w4_codes", align_bytes=64, offset=W4_AT)[:]
@@ -240,7 +241,7 @@ def tile_list_tabts_bias_kernel(tc, tab_words, tab_scales, w4_words, w4_scales, 
                 if 1 <= n <= 3:
                     result = placed.tile([P, CHUNK], F32, name=f"result{n}", offset=RESULTS_AT + 4 * CHUNK * (n - 1))
                 else:
-                    result = keep.tile([P, CHUNK], F32, name=f"result{n}")
+                    result = keep.tile([P, CHUNK], F32, name=f"result{n}", align_bytes=LINE)
                 nc.vector.tensor_tensor(scaled[:], ts_wide[q], sums[q, h][:], MULT)
                 if n == 0:
                     nc.gpsimd.tensor_scalar(result[:], scaled[:], 1.0, bias[:, h : h + 1], MULT, ADD)

@@ -98,9 +98,9 @@ def tile_list_tabts_bias_kernel(tc, tab_words, tab_scales, w4_words, w4_scales, 
             fill=1.0, base=0, channel_multiplier=1,
         )
         nc.vector.memset(ts_window[0 : P - 1, 0 : T // 2], 0.0)
+        nc.vector.memset(ts_window[0 : P - 1, T // 2 : T], 0.0)
         w4_plane = placed.tile([P, M], U8, name="w4_plane", align_bytes=64, offset=W4_PLANE_AT)[:]
         nc.vector.memset(w4_plane.bitcast(I32), 0)
-        nc.vector.memset(ts_window[0 : P - 1, T // 2 : T], 0.0)
 
 
         c_raw = [load_c(0, C0_AT)]
@@ -125,7 +125,7 @@ def tile_list_tabts_bias_kernel(tc, tab_words, tab_scales, w4_words, w4_scales, 
             picked_ts.append(picked)
         first = keep.tile([P, M + CHUNK, PACK], BF16, name="first", align_bytes=64)
         interleave(nc, first[:, 0:M, :], u_raw)
-        picked_scales = placed.tile([P, S], U8, name="picked_scales", align_bytes=64, offset=U_AT + 64)
+        picked_scales = keep.tile([P, S], U8, name="picked_scales", align_bytes=64)
         nc.vector.tensor_copy(picked_scales[:], table_scales[:].indirect(offsets[:]))
 
         first_codes = keep.tile([P, M + CHUNK], U32, name="first_codes", align_bytes=64)

@@ -100,12 +100,13 @@ def tile_list_tabts_bias_kernel(tc, tab_words, tab_scales, w4_words, w4_scales, 
         nc.vector.memset(ts_window[0 : P - 1, 0 : T // 2], 0.0)
         nc.vector.memset(ts_window[0 : P - 1, T // 2 : T], 0.0)
         w4_plane = placed.tile([P, M], U8, name="w4_plane", align_bytes=64, offset=W4_PLANE_AT)[:]
-        nc.vector.memset(w4_plane.bitcast(I32), 0)
+        nc.gpsimd.memset(w4_plane.bitcast(I32), 0)
+        bias_rows = placed.tile([P, P], F32, name="bias_rows", offset=BIAS_ROWS_AT)
+        nc.vector.memset(bias_rows[0 : P - HALVES, :], 0.0)
 
 
         c_raw = [load_c(0, C0_AT)]
 
-        bias_rows = placed.tile([P, P], F32, name="bias_rows", offset=BIAS_ROWS_AT)
         nc.sync.dma_start(out=bias_rows[P - HALVES : P, :], in_=b.rearrange("(h p) -> h p", p=P))
 
         table_words = placed.tile([P, T], I32, name="table_words", align_bytes=LINE, offset=WORDS_AT)
@@ -115,7 +116,6 @@ def tile_list_tabts_bias_kernel(tc, tab_words, tab_scales, w4_words, w4_scales, 
         nc.sync.dma_start(out=w4_codes.bitcast(I32), in_=w4_words[0].bitcast(I32))
         c_raw.append(load_c(1, C1_AT))
         load_scale_rows(nc, w4_plane, w4_scales[0])
-        nc.scalar.copy(out=bias_rows[0 : P - HALVES, :], in_=ident[0 : P - HALVES, :])
 
 
         picked_ts = []

from contextlib import ExitStack

import concourse.mybir as mybir

K, M, T, S = 512, 256, 2048, 1024
FLOPS = 2 * 2 * K * M * S

F32 = mybir.dt.float32
BF16 = mybir.dt.bfloat16
I32 = mybir.dt.int32
U32 = mybir.dt.uint32
U16 = mybir.dt.uint16
U8 = mybir.dt.uint8
FP8X4 = mybir.dt.float8_e4m3fn_x4
FP4X4 = mybir.dt.float4_e2m1fn_x4
MULT = mybir.AluOpType.mult
ADD = mybir.AluOpType.add
IDENT = mybir.ActivationFunctionType.Identity

P = 128
PACK = 4
HALVES = M // P
CHUNK = 256
CHUNKS = S // CHUNK
LAST = CHUNKS - 1
BANK = 512
RAW = 4 * PACK * CHUNK

COLUMNS_AT = 0
C0_AT = COLUMNS_AT + RAW // 2
WIDE_AT = C0_AT + RAW
LINE = 256
C2_AT = WIDE_AT + RAW // 2 + LINE
C3_AT = C2_AT + RAW
RESULTS_AT = C3_AT + RAW
GATE_AT = RESULTS_AT + RAW
C1_AT = GATE_AT + 4 * P
WORDS_AT = C1_AT + RAW
W4_AT = WORDS_AT + 4 * T
W4_PLANE_AT = W4_AT + 2 * M
BIAS_ROWS_AT = W4_PLANE_AT + M
GATE_END = BIAS_ROWS_AT + 4 * P
PICKED_AT = GATE_END
U_AT = PICKED_AT + 4 * 4 * CHUNK
SUM_BANKS = (2, 4, 6, 0)
SHARE = 64


def load_scale_rows(nc, plane, rows):
    for r in range(4):
        nc.sync.dma_start(out=plane[r:P:32, :].bitcast(I32), in_=rows[r:16:4, :].bitcast(I32))


def interleave(nc, grouped, raw):
    nc.scalar.copy(
        out=grouped.rearrange("p (c i) t -> p c t i", i=2),
        in_=raw.rearrange("p t (c i) -> p c t i", i=2),
    )


def tile_list_tabts_bias_kernel(tc, tab_words, tab_scales, w4_words, w4_scales, c, u, ts, b, offs, out):
    nc = tc.nc
    with ExitStack() as ctx:
        keep = ctx.enter_context(tc.tile_pool(name="keep", bufs=1))
        placed = ctx.enter_context(tc.tile_pool(name="placed", bufs=1))
        psum = ctx.enter_context(tc.psum_pool(name="psum", bufs=1))

        offsets = keep.tile([P, S // 16], U16, name="offsets")
        nc.sync.dma_start(offsets[:], offs)

        ts_window = keep.tile([P, T], F32, name="ts_window", align_bytes=LINE)
        nc.sync.dma_start(out=ts_window[P - 1 : P, :], in_=ts[0:1, :])

        u_raw = placed.tile([P, PACK, M], F32, name="u_raw", offset=U_AT)[:]
        nc.sync.dma_start(out=u_raw, in_=u.rearrange("(p t) n -> p t n", t=PACK))

        c_rows = c.rearrange("(p t) j -> p t j", t=PACK)

        def load_c(q, at):
            rim = {0: (RAW // 2 + LINE) // 4, 3: RAW // 4}.get(q, 0)
            tile = placed.tile([P, PACK * CHUNK + rim], F32, name=f"c_raw{q}", offset=at)
            raw = tile[:, 0 : PACK * CHUNK].rearrange("p (t j) -> p t j", t=PACK)
            width = P if q == LAST else CHUNK
            for j in range(0, CHUNK, width):
                nc.sync.dma_start(out=raw[:, :, j : j + width], in_=c_rows[:, :, q * CHUNK + j : q * CHUNK + j + width])
            return raw

        table_scales = keep.tile([P, T], U8, name="table_scales", align_bytes=LINE)
        nc.vector.memset(table_scales[:].bitcast(I32), 0)
        load_scale_rows(nc, table_scales, tab_scales[0])

        gate = placed.tile([P, (GATE_END - C0_AT) // 4], F32, name="gate", offset=C0_AT)
        zeros = gate[:, (GATE_AT - C0_AT) // 4 : (GATE_AT - C0_AT) // 4 + P]
        nc.vector.memset(zeros, 0.0)
        ident = keep.tile([P, P], F32, name="ident")
        nc.gpsimd.affine_select(
            out=ident[:], in_=zeros, pattern=[[-1, P]], compare_op=mybir.AluOpType.not_equal,
            fill=1.0, base=0, channel_multiplier=1,
        )
        nc.vector.memset(ts_window[0 : P - 1, 0 : T // 2], 0.0)
        nc.vector.memset(ts_window[0 : P - 1, T // 2 : T], 0.0)
        w4_plane = placed.tile([P, M], U8, name="w4_plane", align_bytes=64, offset=W4_PLANE_AT)[:]
        nc.gpsimd.memset(w4_plane.bitcast(I32), 0)
        bias_rows = placed.tile([P, P], F32, name="bias_rows", offset=BIAS_ROWS_AT)
        nc.vector.memset(bias_rows[0 : P - HALVES, :], 0.0)


        c_raw = [load_c(0, C0_AT)]

        nc.sync.dma_start(out=bias_rows[P - HALVES : P, :], in_=b.rearrange("(h p) -> h p", p=P))

        table_words = placed.tile([P, T], I32, name="table_words", align_bytes=LINE, offset=WORDS_AT)
        nc.sync.dma_start(out=table_words[:], in_=tab_words[0].rearrange("p t i -> p (t i)").bitcast(I32))

        w4_codes = placed.tile([P, 2 * M], U8, name="w4_codes", align_bytes=64, offset=W4_AT)[:]
        nc.sync.dma_start(out=w4_codes.bitcast(I32), in_=w4_words[0].bitcast(I32))
        c_raw.append(load_c(1, C1_AT))
        load_scale_rows(nc, w4_plane, w4_scales[0])


        picked_ts = []
        for g in range(2):
            picked = keep.tile([P, BANK], F32, name=f"picked_ts{g}")
            nc.vector.tensor_copy(picked[:], ts_window[:].indirect(offsets[:, g * BANK // 16 : (g + 1) * BANK // 16]))
            picked_ts.append(picked)
        first = keep.tile([P, M + CHUNK, PACK], BF16, name="first", align_bytes=64)
        interleave(nc, first[:, 0:M, :], u_raw)
        picked_scales = keep.tile([P, S], U8, name="picked_scales", align_bytes=64)
        nc.vector.tensor_copy(picked_scales[:], table_scales[:].indirect(offsets[:]))

        first_codes = keep.tile([P, M + CHUNK], U32, name="first_codes", align_bytes=64)
        first_plane = keep.tile([P, M + CHUNK], U8, name="first_plane", align_bytes=64)
        c_codes = [first_codes[:, M : M + CHUNK]]
        c_planes = [first_plane[:, M : M + CHUNK]]

        def round_c(q):
            grouped = placed.tile([P, CHUNK, PACK], BF16, name=f"c_grouped{q}", align_bytes=64, offset=COLUMNS_AT + (q - 1) * RAW // 2)
            if q < LAST:
                interleave(nc, grouped[:], c_raw[q])
            else:
                cut = CHUNK - SHARE
                interleave(nc, grouped[:, 0:P, :], c_raw[q][:, :, 0:P])
                interleave(nc, grouped[:, P:cut, :], c_raw[q][:, :, P:cut])
                nc.gpsimd.tensor_scalar(grouped[:, cut:CHUNK, :], c_raw[q][:, :, cut:CHUNK].rearrange("p t j -> p j t"), 1.0, 0.0, MULT, ADD)
            return grouped

        def quantise_c(q, grouped):
            if q == 1:
                codes = placed.tile([P, CHUNK], U32, name="c_codes1", align_bytes=64, offset=PICKED_AT + 3 * 4 * CHUNK)
            else:
                codes = keep.tile([P, CHUNK], U32, name=f"c_codes{q}", align_bytes=64)
            plane = keep.tile([P, CHUNK], U8, name=f"c_plane{q}", align_bytes=64)
            nc.vector.quantize_mx(out=codes[:].bitcast(FP8X4), scales=plane[:], in_=grouped[:].rearrange("p j t -> p (j t)"))
            c_codes.append(codes[:])
            c_planes.append(plane[:])

        bias_turned = psum.tile([P, P], F32, name="bias_turned", tag="bank7")
        nc.tensor.transpose(bias_turned[:], bias_rows[:], ident[:])

        ts_wide = []

        def turn_ts(g):
            turned = psum.tile([P, 4, P], F32, name=f"turned{g}", tag=f"bank{g}")
            for i in range(4):
                nc.tensor.transpose(turned[:, i, :], picked_ts[g][:, i * P : (i + 1) * P], ident[:])
            if g == 0:
                columns = placed.tile([P, 4], F32, name="columns0", offset=U_AT)[:]
            else:
                columns = placed.tile([P, (RAW + 32) // 4], F32, name="columns1", offset=COLUMNS_AT)[:, 0:4]
            nc.scalar.copy(out=columns, in_=turned[:, :, P - 1])
            return columns

        def spread_ts(g, columns):
            for q in range(2 * g, 2 * g + 2):
                spread = psum.tile([P, 2, P], F32, name=f"spread{q}", tag=f"bank{2 + q}")
                for i in range(2):
                    col = 2 * (q % 2) + i
                    nc.tensor.transpose(spread[:, i, :], columns[:, col : col + 1].to_broadcast([P, P]), ident[:])
                if g == 0:
                    wide = placed.tile([P, CHUNK], F32, name=f"ts_wide{q}", offset=WIDE_AT + 4 * CHUNK * q)
                else:
                    wide = keep.tile([P, CHUNK], F32, name=f"ts_wide{q}")
                nc.scalar.copy(out=wide[:], in_=spread[:].rearrange("m i p -> m (i p)"))
                ts_wide.append(wide[:])

        columns0 = turn_ts(0)
        interleave(nc, first[:, M : M + CHUNK, :], c_raw[0])
        nc.vector.quantize_mx(out=first_codes[:].bitcast(FP8X4), scales=first_plane[:], in_=first[:].rearrange("p n t -> p (n t)"))
        columns1 = turn_ts(1)
        spread_ts(0, columns0)
        bias = placed.tile([P, HALVES], F32, name="bias", offset=C2_AT - 32)[:]
        nc.scalar.copy(out=bias, in_=bias_turned[:, P - HALVES : P])
        spread_ts(1, columns1)
        grouped1 = round_c(1)
        c_raw.append(load_c(2, C2_AT))
        c_raw.append(load_c(3, C3_AT))

        sums = {}
        picked_words = {}

        def open_sums(q):
            for h in range(HALVES):
                sums[q, h] = psum.tile([P, CHUNK], F32, name=f"acc{q}{h}", tag=f"bank{SUM_BANKS[q] + h}")

        def pick_words(q):
            picked = placed.tile([P, 2 * CHUNK if q == 0 else CHUNK], U32, name=f"picked_words{q}", align_bytes=64, offset=PICKED_AT + 4 * CHUNK * (2, 0, 1, 2)[q])[:, 0:CHUNK]
            nc.vector.tensor_copy(picked, table_words[:].bitcast(U32).indirect(offsets[:, q * CHUNK // 16 : (q + 1) * CHUNK // 16]))
            picked_words[q] = picked

        def table_passes(q, opens):
            for h in range(HALVES):
                nc.tensor.matmul_mx(
                    out=sums[q, h][:],
                    lhsT=w4_codes[:, 2 * P * h : 2 * P * (h + 1)].bitcast(FP4X4),
                    lhsT_scale=w4_plane[:, P * h : P * (h + 1)],
                    rhs=picked_words[q].bitcast(FP8X4),
                    rhs_scale=picked_scales[:, q * CHUNK : (q + 1) * CHUNK],
                    start=opens,
                    stop=not opens,
                )

        def c_passes(q, opens):
            for h in range(HALVES):
                nc.tensor.matmul_mx(
                    out=sums[q, h][:],
                    lhsT=first_codes[:, P * h : P * (h + 1)].bitcast(FP8X4),
                    lhsT_scale=first_plane[:, P * h : P * (h + 1)],
                    rhs=c_codes[q].bitcast(FP8X4),
                    rhs_scale=c_planes[q],
                    start=opens,
                    stop=not opens,
                )

        def finish(q):
            for h in range(HALVES):
                n = q * HALVES + h
                if q == 2:
                    scaled = placed.tile([P, CHUNK], F32, name=f"scaled{n}", offset=C3_AT + 4 * CHUNK * (1 + h))
                else:
                    scaled = keep.tile([P, CHUNK], F32, name=f"scaled{n}")
                if 1 <= n <= 3:
                    result = placed.tile([P, CHUNK], F32, name=f"result{n}", offset=RESULTS_AT + 4 * CHUNK * (n - 1))
                else:
                    result = keep.tile([P, CHUNK], F32, name=f"result{n}", align_bytes=LINE)
                nc.vector.tensor_tensor(scaled[:], ts_wide[q], sums[q, h][:], MULT)
                if n == 0:
                    nc.gpsimd.tensor_scalar(result[:], scaled[:], 1.0, bias[:, h : h + 1], MULT, ADD)
                else:
                    nc.scalar.activation(result[:], scaled[:], IDENT, bias=bias[:, h : h + 1])
                queue = nc.scalar if n == CHUNKS * HALVES - 1 else nc.sync
                queue.dma_start(out=out[h * P : (h + 1) * P, q * CHUNK : (q + 1) * CHUNK], in_=result[:])

        open_sums(0)
        c_passes(0, True)
        pick_words(0)
        table_passes(0, False)
        open_sums(1)
        pick_words(1)
        table_passes(1, True)
        pick_words(2)
        grouped2 = round_c(2)
        grouped3 = round_c(3)
        finish(0)
        quantise_c(1, grouped1)
        c_passes(1, False)
        open_sums(2)
        table_passes(2, True)
        pick_words(3)
        open_sums(LAST)
        table_passes(LAST, True)
        finish(1)
        quantise_c(2, grouped2)
        c_passes(2, False)
        for k in range(2):
            codes = keep.tile([P, P], U32, name=f"last_codes{k}", align_bytes=64)
            plane = keep.tile([P, P], U8, name=f"last_plane{k}", align_bytes=64)
            nc.vector.quantize_mx(out=codes[:].bitcast(FP8X4), scales=plane[:], in_=grouped3[:, k * P : (k + 1) * P, :].rearrange("p j t -> p (j t)"))
            for h in range(HALVES):
                nc.tensor.matmul_mx(
                    out=sums[LAST, h][:, k * P : (k + 1) * P],
                    lhsT=first_codes[:, P * h : P * (h + 1)].bitcast(FP8X4),
                    lhsT_scale=first_plane[:, P * h : P * (h + 1)],
                    rhs=codes[:].bitcast(FP8X4),
                    rhs_scale=plane[:],
                    start=False,
                    stop=(k == 1),
                )
        finish(2)
        finish(LAST)
